import numpy as np
import ml_dtypes


def mxq(x, axis, fmt="e4m3"):
    dtype, down = {"e4m3": (ml_dtypes.float8_e4m3fn, 7), "e5m2": (ml_dtypes.float8_e5m2, 14)}[fmt]
    v = np.moveaxis(np.asarray(x, np.float32).astype(ml_dtypes.bfloat16).astype(np.float64), axis, -1)
    blocks = v.reshape(v.shape[:-1] + (-1, 32))
    amax = np.abs(blocks).max(-1, keepdims=True)
    byte = np.maximum(np.where(amax > 0, np.frexp(amax)[1] - 1 + 127, 0) - down, 1)
    scale = np.exp2(byte - 127.0)
    codes = (blocks / scale).astype(np.float32).astype(dtype).astype(np.float64)
    return np.moveaxis((codes * scale).reshape(v.shape), -1, axis)


WIDE = False


def mx_kscale(k):
    if not WIDE:
        return np.ones(k)
    levels = np.array([10, -10, 5, -5, 0])
    if k % 512:
        return np.exp2(np.random.permutation(np.resize(levels, k // 32))).repeat(32)
    a = np.empty((k // 512, 16))
    for p in range(k // 512):
        a[p, :8] = np.random.permutation(np.resize(levels, 8))
        for g in range(8):
            far = levels[np.abs(levels - a[p, g]) >= 10]
            a[p, g + 8] = far[np.random.randint(len(far))]
    return np.exp2(a.ravel()).repeat(32)


def f64(x):
    return np.asarray(x).astype(np.float64)


def striped(idx):
    return np.tile(idx.reshape(-1, 16).T, (8, 1)).astype(np.uint16)


def unstriped(offs):
    return offs[:16].T.reshape(-1).astype(np.int64)


E2M1 = np.array([0.0, 0.5, 1.0, 1.5, 2.0, 3.0, 4.0, 6.0, -0.0, -0.5, -1.0, -1.5, -2.0, -3.0, -4.0, -6.0])


def pack_weight(w, fmt):
    k, n = w.shape
    w = f64(np.asarray(w, np.float32).astype(ml_dtypes.bfloat16)).reshape(k // 32, 32, n)
    amax = np.abs(w).max(1)
    if fmt == "e4m3":
        byte = np.frexp(amax)[1] - 1 + 127 - 7
    else:
        mant, ex = np.frexp(amax / 6.0)
        byte = np.where(mant > 0.5, ex, ex - 1) + 127
    byte = np.clip(np.where(amax > 0, byte, 1), 1, 254)
    scaled = (w * np.exp2(127.0 - byte)[:, None, :]).reshape(k, n).astype(np.float32)
    by_word = np.ascontiguousarray(scaled.reshape(k // 512, 128, 4, n).transpose(0, 1, 3, 2))
    if fmt == "e4m3":
        words = by_word.astype(ml_dtypes.float8_e4m3fn).view(np.uint8)
    else:
        c = by_word.astype(ml_dtypes.float4_e2m1fn).view(np.uint8) & 0xF
        words = (c[..., 0::2] | (c[..., 1::2] << 4)).reshape(k // 512, 128, 2 * n)
    return np.ascontiguousarray(words), np.ascontiguousarray(byte.astype(np.uint8).reshape(k // 512, 16, n))


def unpack_weight(words, scales, fmt):
    g, _, n = scales.shape
    words = np.ascontiguousarray(words).reshape(g, 128, n, -1)
    if fmt == "e4m3":
        vals = words.view(ml_dtypes.float8_e4m3fn).astype(np.float64)
    else:
        nib = np.empty((g, 128, n, 4), np.uint8)
        nib[..., 0::2] = words & 0xF
        nib[..., 1::2] = words >> 4
        vals = E2M1[nib]
    vals = vals * np.repeat(np.exp2(scales.astype(np.float64) - 127.0), 8, axis=1)[..., None]
    return vals.transpose(0, 1, 3, 2).reshape(g * 512, n)


def pack_table4(v):
    words, scales = pack_weight(v, "e2m1")
    g, t = words.shape[0] // 2, v.shape[1]
    words = words.reshape(g, 2, 128, t, 2).transpose(0, 2, 3, 1, 4)
    return np.concatenate([words.reshape(g, -1), scales.reshape(g, -1)], axis=1)


def unpack_table4(tab):
    g, t = tab.shape[0], tab.shape[1] // 544
    words = tab[:, :512 * t].reshape(g, 128, t, 2, 2).transpose(0, 3, 1, 2, 4).reshape(2 * g, 128, 2 * t)
    return unpack_weight(words, tab[:, 512 * t:].reshape(2 * g, 16, t), "e2m1")


def pack_table(v):
    words, scales = pack_weight(v, "e4m3")
    return np.concatenate([words.reshape(words.shape[0], -1), scales.reshape(scales.shape[0], -1)], axis=1)


def unpack_table(tab):
    g, t = tab.shape[0], tab.shape[1] // 528
    return unpack_weight(tab[:, :512 * t].reshape(g, 128, t, 4), tab[:, 512 * t:].reshape(g, 16, t), "e4m3")


def gelu(v):
    return 0.5 * v * (1.0 + np.tanh(np.sqrt(2.0 / np.pi) * (v + 0.044715 * v**3)))


K, L, M, T, S = 1024, 1024, 128, 2048, 1024


def setup_inputs():
    n = np.random.standard_normal
    s1 = mx_kscale(K)[:, None]
    s2 = mx_kscale(L)[:, None]
    p_w4 = pack_weight(n((K, M)) / np.sqrt(K) / s1, "e2m1")
    return {
        "tab": pack_table(n((K, T)) * s1),
        "w4_words": p_w4[0],
        "w4_scales": p_w4[1],
        "tab2": pack_table4(n((L, T)) * s2),
        "u": (n((L, M)) / np.sqrt(L) / s2).astype(np.float32),
        "b": (0.3 * n(128)).astype(np.float32),
        "offs": striped(np.random.permutation(T)[:S]),
        "offs2": striped(np.random.permutation(T)[:S]),
    }


def reference(tab, w4_words, w4_scales, tab2, u, b, offs, offs2):
    tab_ = unpack_table(tab)[:, unstriped(offs)]
    w4_ = unpack_weight(w4_words, w4_scales, "e2m1")
    tab2_ = unpack_table4(tab2)[:, unstriped(offs2)]
    u_ = mxq(f64(u), 0, "e4m3")
    y = w4_.T @ tab_ + u_.T @ tab2_
    return gelu(y + f64(b)[:, None])

@@ -1,0 +1,137 @@
+from contextlib import ExitStack
+
+import concourse.mybir as mybir
+
+K, L, M, T, S = 1024, 1024, 128, 2048, 1024
+FLOPS = 2 * (K + L) * M * S
+
+F32 = mybir.dt.float32
+BF16 = mybir.dt.bfloat16
+I32 = mybir.dt.int32
+U32 = mybir.dt.uint32
+U16 = mybir.dt.uint16
+U8 = mybir.dt.uint8
+FP8X4 = mybir.dt.float8_e4m3fn_x4
+FP4X4 = mybir.dt.float4_e2m1fn_x4
+GELU = mybir.ActivationFunctionType.Gelu_apprx_tanh
+
+P = 128
+PACK = 4
+PASSES = 2
+QUADS = 4
+QUAD = 32
+LIVE = 4
+STRIPE = 16
+WORD_BYTES = P * PACK * T
+
+GROUPS = [(0, 512), (512, 640), (640, 768), (768, 896), (896, 1024)]
+CHUNKS = [(0, 512), (512, 768), (768, 1024)]
+
+
+def tile_list_tab48_gelu_kernel(tc, tab, w4_words, w4_scales, tab2, u, b, offs, offs2, out):
+    nc = tc.nc
+    with ExitStack() as ctx:
+        keep = ctx.enter_context(tc.tile_pool(name="keep", bufs=1))
+        psum = ctx.enter_context(tc.psum_pool(name="psum", bufs=1))
+
+        list8 = keep.tile([P, S // STRIPE], U16, name="list8")
+        list4 = keep.tile([P, S // STRIPE], U16, name="list4")
+        rows4 = keep.tile([P, T // 4], I32, name="rows4", align_bytes=64)
+        rows8 = keep.tile([P, PASSES, T // 4], I32, name="rows8", align_bytes=64)
+        words4 = keep.tile([P, T], I32, name="words4", align_bytes=64)
+        words8 = [keep.tile([P, T], I32, name=f"words8_{a}", align_bytes=64) for a in range(PASSES)]
+        u_raw = keep.tile([P, PASSES, PACK, M], F32, name="u_raw", align_bytes=64)
+        u_bf = keep.tile([P, PASSES, M, PACK], BF16, name="u_bf", align_bytes=64)
+        u_codes = keep.tile([P, PASSES * M], U32, name="u_codes", align_bytes=64)
+        u_scales = keep.tile([P, PASSES * M], U8, name="u_scales", align_bytes=64)
+        w_words = keep.tile([P, PASSES, 2 * M // 4], I32, name="w_words", align_bytes=64)
+        w_scales = keep.tile([P, PASSES, M // 4], I32, name="w_scales", align_bytes=64)
+        bias = keep.tile([P, 1], F32, name="bias")
+        warm = keep.tile([P, 1], F32, name="warm")
+        warm_out = keep.tile([P, 1], F32, name="warm_out")
+        got_rows4 = keep.tile([P, S], U8, name="got_rows4", align_bytes=64)
+        plane4 = keep.tile([P, PASSES, S // 4], I32, name="plane4", align_bytes=64)
+        plane8 = keep.tile([P, PASSES, S], U8, name="plane8", align_bytes=64)
+        got4 = keep.tile([P, S], U32, name="got4", align_bytes=64)
+        parted4 = keep.tile([P, PASSES, S], U16, name="parted4", align_bytes=64)
+        got8 = [keep.tile([P, S], U32, name=f"got8_{a}", align_bytes=64) for a in range(PASSES)]
+        result = keep.tile([P, S], F32, name="result", align_bytes=64)
+        acc = [psum.tile([P, hi - lo], F32, name=f"acc{g}") for g, (lo, hi) in enumerate(GROUPS)]
+
+        first4 = P - PASSES * QUADS * LIVE
+        tab_scales = tab[:, WORD_BYTES:].rearrange("a (q t) -> q a t", t=T).bitcast(I32)
+        tab2_scales = tab2[0, WORD_BYTES:].rearrange("(q t) -> q t", t=T).bitcast(I32)
+        w4_scale_rows = w4_scales.rearrange("a q n -> q a n").bitcast(I32)
+
+        nc.scalar.dma_start(rows4[first4:P, :], tab2_scales)
+        nc.sync.dma_start(list4[:], offs2)
+        nc.vector.memset(rows8[:], 0)
+        nc.vector.memset(rows4[0:first4, :], 0)
+        nc.vector.memset(w_scales[:], 0)
+        nc.vector.memset(plane4[:], 0)
+        nc.vector.memset(warm[:], 0.0)
+        nc.scalar.activation(warm_out[:], warm[:], GELU)
+
+        nc.sync.dma_start(list8[:], offs)
+        for q in range(QUADS):
+            nc.sync.dma_start(rows8[QUAD * q : QUAD * q + LIVE, :, :], tab_scales[LIVE * q : LIVE * (q + 1)])
+        nc.sync.dma_start(words4[:], tab2[0, 0:WORD_BYTES].rearrange("(p w) -> p w", p=P).bitcast(I32))
+        nc.sync.dma_start(u_raw[:], u.rearrange("(a p i) n -> p a i n", p=P, i=PACK))
+        for a in range(PASSES):
+            nc.sync.dma_start(words8[a][:], tab[a, 0:WORD_BYTES].rearrange("(p w) -> p w", p=P).bitcast(I32))
+        nc.sync.dma_start(w_words[:], w4_words.rearrange("a p n -> p a n").bitcast(I32))
+        for q in range(QUADS):
+            nc.sync.dma_start(w_scales[QUAD * q : QUAD * q + LIVE, :, :], w4_scale_rows[LIVE * q : LIVE * (q + 1)])
+        nc.sync.dma_start(bias[:], b.rearrange("(p o) -> p o", o=1))
+
+        nc.vector.tensor_copy(got_rows4[:], rows4[:].bitcast(U8).indirect(list4[:]))
+        for h in range(PASSES):
+            for q in range(QUADS):
+                row = first4 + LIVE * (QUADS * h + q)
+                nc.sync.dma_start(plane4[QUAD * q : QUAD * q + LIVE, h, :], got_rows4[row : row + LIVE, :].bitcast(I32))
+        for a in range(PASSES):
+            nc.vector.tensor_copy(plane8[:, a, :], rows8[:, a, :].bitcast(U8).indirect(list8[:]))
+
+        nc.scalar.copy(u_bf[:], u_raw[:].rearrange("p a i n -> p a n i"))
+        nc.vector.tensor_copy(got4[:], words4[:].bitcast(U32).indirect(list4[:]))
+        nc.vector.quantize_mx(
+            out=u_codes[:].bitcast(FP8X4), scales=u_scales[:], in_=u_bf[:].rearrange("p a n i -> p (a n i)")
+        )
+        nc.vector.tensor_copy(parted4[:], got4[:].bitcast(U16).rearrange("p (j h) -> p h j", h=PASSES))
+        for h in range(PASSES):
+            for g, (lo, hi) in enumerate(GROUPS):
+                nc.tensor.matmul_mx(
+                    out=acc[g][:],
+                    lhsT=u_codes[:, h * M : (h + 1) * M].bitcast(FP8X4),
+                    lhsT_scale=u_scales[:, h * M : (h + 1) * M],
+                    rhs=parted4[:, h, lo:hi].bitcast(FP4X4),
+                    rhs_scale=plane4[:, h, :].bitcast(U8)[:, lo:hi],
+                    start=(h == 0),
+                    stop=False,
+                )
+
+        def table8_pass(a, g):
+            lo, hi = GROUPS[g]
+            nc.tensor.matmul_mx(
+                out=acc[g][:],
+                lhsT=w_words[:, a, :].bitcast(FP4X4),
+                lhsT_scale=w_scales[:, a, :].bitcast(U8),
+                rhs=got8[a][:, lo:hi].bitcast(FP8X4),
+                rhs_scale=plane8[:, a, lo:hi],
+                start=False,
+                stop=(a == PASSES - 1),
+            )
+
+        nc.vector.tensor_copy(got8[0][:], words8[0][:].bitcast(U32).indirect(list8[:]))
+        for g in range(len(GROUPS)):
+            table8_pass(0, g)
+
+        for c0, c1 in CHUNKS:
+            nc.vector.tensor_copy(
+                got8[1][:, c0:c1], words8[1][:].bitcast(U32).indirect(list8[:, c0 // STRIPE : c1 // STRIPE])
+            )
+            for g, (lo, hi) in enumerate(GROUPS):
+                if c0 <= lo < c1:
+                    table8_pass(1, g)
+                    nc.scalar.activation(result[:, lo:hi], acc[g][:], GELU, bias=bias[:])
+            nc.sync.dma_start(out[:, c0:c1], result[:, c0:c1])

@@ -25,7 +25,8 @@ STRIPE = 16
 WORD_BYTES = P * PACK * T
 
 GROUPS = [(0, 512), (512, 640), (640, 768), (768, 896), (896, 1024)]
-CHUNKS = [(0, 512), (512, 768), (768, 1024)]
+GATHERS8 = [(0, 0, 512), (1, 0, 512), (0, 512, 1024), (1, 512, 768), (1, 768, 1024)]
+STORE_FROM = {512: 0, 768: 512, 896: 768}
 
 
 def tile_list_tab48_gelu_kernel(tc, tab, w4_words, w4_scales, tab2, u, b, offs, offs2, out):
@@ -39,8 +40,11 @@ def tile_list_tab48_gelu_kernel(tc, tab, w4_words, w4_scales, tab2, u, b, offs, 
         rows4 = keep.tile([P, T // 4], I32, name="rows4", align_bytes=64)
         rows8 = keep.tile([P, PASSES, T // 4], I32, name="rows8", align_bytes=64)
         words4 = keep.tile([P, T], I32, name="words4", align_bytes=64)
-        words8 = [keep.tile([P, T], I32, name=f"words8_{a}", align_bytes=64) for a in range(PASSES)]
-        u_raw = keep.tile([P, PASSES, PACK, M], F32, name="u_raw", align_bytes=64)
+        u_raw = keep.tile([P, PASSES, PACK, M], F32, name="u_raw", tag="shared", align_bytes=64)
+        words8 = [
+            keep.tile([P, T], I32, name="words8_0", align_bytes=64),
+            keep.tile([P, T], I32, name="words8_1", tag="shared", align_bytes=64),
+        ]
         u_bf = keep.tile([P, PASSES, M, PACK], BF16, name="u_bf", align_bytes=64)
         u_codes = keep.tile([P, PASSES * M], U32, name="u_codes", align_bytes=64)
         u_scales = keep.tile([P, PASSES * M], U8, name="u_scales", align_bytes=64)
@@ -77,12 +81,11 @@ def tile_list_tab48_gelu_kernel(tc, tab, w4_words, w4_scales, tab2, u, b, offs, 
             nc.sync.dma_start(rows8[QUAD * q : QUAD * q + LIVE, :, :], tab_scales[LIVE * q : LIVE * (q + 1)])
         nc.sync.dma_start(words4[:], tab2[0, 0:WORD_BYTES].rearrange("(p w) -> p w", p=P).bitcast(I32))
         nc.sync.dma_start(u_raw[:], u.rearrange("(a p i) n -> p a i n", p=P, i=PACK))
-        for a in range(PASSES):
-            nc.sync.dma_start(words8[a][:], tab[a, 0:WORD_BYTES].rearrange("(p w) -> p w", p=P).bitcast(I32))
-        nc.sync.dma_start(w_words[:], w4_words.rearrange("a p n -> p a n").bitcast(I32))
+        nc.sync.dma_start(words8[0][:], tab[0, 0:WORD_BYTES].rearrange("(p w) -> p w", p=P).bitcast(I32))
+        nc.scalar.dma_start(w_words[:], w4_words.rearrange("a p n -> p a n").bitcast(I32))
         for q in range(QUADS):
-            nc.sync.dma_start(w_scales[QUAD * q : QUAD * q + LIVE, :, :], w4_scale_rows[LIVE * q : LIVE * (q + 1)])
-        nc.sync.dma_start(bias[:], b.rearrange("(p o) -> p o", o=1))
+            nc.scalar.dma_start(w_scales[QUAD * q : QUAD * q + LIVE, :, :], w4_scale_rows[LIVE * q : LIVE * (q + 1)])
+        nc.scalar.dma_start(bias[:], b.rearrange("(p o) -> p o", o=1))
 
         nc.vector.tensor_copy(got_rows4[:], rows4[:].bitcast(U8).indirect(list4[:]))
         for h in range(PASSES):
@@ -93,13 +96,14 @@ def tile_list_tab48_gelu_kernel(tc, tab, w4_words, w4_scales, tab2, u, b, offs, 
             nc.vector.tensor_copy(plane8[:, a, :], rows8[:, a, :].bitcast(U8).indirect(list8[:]))
 
         nc.scalar.copy(u_bf[:], u_raw[:].rearrange("p a i n -> p a n i"))
+        nc.sync.dma_start(words8[1][:], tab[1, 0:WORD_BYTES].rearrange("(p w) -> p w", p=P).bitcast(I32))
         nc.vector.tensor_copy(got4[:], words4[:].bitcast(U32).indirect(list4[:]))
         nc.vector.quantize_mx(
             out=u_codes[:].bitcast(FP8X4), scales=u_scales[:], in_=u_bf[:].rearrange("p a n i -> p (a n i)")
         )
         nc.vector.tensor_copy(parted4[:], got4[:].bitcast(U16).rearrange("p (j h) -> p h j", h=PASSES))
-        for h in range(PASSES):
-            for g, (lo, hi) in enumerate(GROUPS):
+        for g, (lo, hi) in enumerate(GROUPS):
+            for h in range(PASSES):
                 nc.tensor.matmul_mx(
                     out=acc[g][:],
                     lhsT=u_codes[:, h * M : (h + 1) * M].bitcast(FP8X4),
@@ -122,16 +126,16 @@ def tile_list_tab48_gelu_kernel(tc, tab, w4_words, w4_scales, tab2, u, b, offs, 
                 stop=(a == PASSES - 1),
             )
 
-        nc.vector.tensor_copy(got8[0][:], words8[0][:].bitcast(U32).indirect(list8[:]))
-        for g in range(len(GROUPS)):
-            table8_pass(0, g)
-
-        for c0, c1 in CHUNKS:
+        for a, c0, c1 in GATHERS8:
             nc.vector.tensor_copy(
-                got8[1][:, c0:c1], words8[1][:].bitcast(U32).indirect(list8[:, c0 // STRIPE : c1 // STRIPE])
+                got8[a][:, c0:c1], words8[a][:].bitcast(U32).indirect(list8[:, c0 // STRIPE : c1 // STRIPE])
             )
             for g, (lo, hi) in enumerate(GROUPS):
                 if c0 <= lo < c1:
-                    table8_pass(1, g)
-                    nc.scalar.activation(result[:, lo:hi], acc[g][:], GELU, bias=bias[:])
-            nc.sync.dma_start(out[:, c0:c1], result[:, c0:c1])
+                    table8_pass(a, g)
+                    if a == PASSES - 1:
+                        nc.scalar.activation(result[:, lo:hi], acc[g][:], GELU, bias=bias[:])
+                        if hi == S:
+                            nc.scalar.dma_start(out[:, lo:hi], result[:, lo:hi])
+                        elif hi in STORE_FROM:
+                            nc.sync.dma_start(out[:, STORE_FROM[hi] : hi], result[:, STORE_FROM[hi] : hi])

@@ -25,6 +25,7 @@ STRIPE = 16
 WORD_BYTES = P * PACK * T
 
 GROUPS = [(0, 512), (512, 640), (640, 768), (768, 896), (896, 1024)]
+HALVES = [(0, 512), (512, 1024)]
 GATHERS8 = [(0, 0, 512), (1, 0, 512), (0, 512, 1024), (1, 512, 768), (1, 768, 1024)]
 STORE_FROM = {512: 0, 768: 512, 896: 768}
 
@@ -39,13 +40,13 @@ def tile_list_tab48_gelu_kernel(tc, tab, w4_words, w4_scales, tab2, u, b, offs, 
         list4 = keep.tile([P, S // STRIPE], U16, name="list4")
         rows4 = keep.tile([P, T // 4], I32, name="rows4", align_bytes=64)
         rows8 = keep.tile([P, PASSES, T // 4], I32, name="rows8", align_bytes=64)
-        words4 = keep.tile([P, T], I32, name="words4", align_bytes=64)
+        words4 = keep.tile([P, T], I32, name="words4", tag="after_words4", align_bytes=64)
         u_raw = keep.tile([P, PASSES, PACK, M], F32, name="u_raw", tag="shared", align_bytes=64)
         words8 = [
             keep.tile([P, T], I32, name="words8_0", align_bytes=64),
             keep.tile([P, T], I32, name="words8_1", tag="shared", align_bytes=64),
         ]
-        u_bf = keep.tile([P, PASSES, M, PACK], BF16, name="u_bf", align_bytes=64)
+        u_bf = keep.tile([P, PASSES, M, PACK], BF16, name="u_bf", tag="after_u_bf", align_bytes=64)
         u_codes = keep.tile([P, PASSES * M], U32, name="u_codes", align_bytes=64)
         u_scales = keep.tile([P, PASSES * M], U8, name="u_scales", align_bytes=64)
         w_words = keep.tile([P, PASSES, 2 * M // 4], I32, name="w_words", align_bytes=64)
@@ -55,7 +56,10 @@ def tile_list_tab48_gelu_kernel(tc, tab, w4_words, w4_scales, tab2, u, b, offs, 
         warm_out = keep.tile([P, 1], F32, name="warm_out")
         got_rows4 = keep.tile([P, S], U8, name="got_rows4", align_bytes=64)
         plane4 = keep.tile([P, PASSES, S // 4], I32, name="plane4", align_bytes=64)
-        plane8 = keep.tile([P, PASSES, S], U8, name="plane8", align_bytes=64)
+        plane8 = [
+            keep.tile([P, S], U8, name="plane8_0", tag="after_words4", align_bytes=64),
+            keep.tile([P, S], U8, name="plane8_1", tag="after_u_bf", align_bytes=64),
+        ]
         got4 = keep.tile([P, S], U32, name="got4", align_bytes=64)
         parted4 = keep.tile([P, PASSES, S], U16, name="parted4", align_bytes=64)
         got8 = [keep.tile([P, S], U32, name=f"got8_{a}", align_bytes=64) for a in range(PASSES)]
@@ -67,19 +71,24 @@ def tile_list_tab48_gelu_kernel(tc, tab, w4_words, w4_scales, tab2, u, b, offs, 
         tab2_scales = tab2[0, WORD_BYTES:].rearrange("(q t) -> q t", t=T).bitcast(I32)
         w4_scale_rows = w4_scales.rearrange("a q n -> q a n").bitcast(I32)
 
-        nc.scalar.dma_start(rows4[first4:P, :], tab2_scales)
+        nc.sync.dma_start(rows4[first4:P, :], tab2_scales)
         nc.sync.dma_start(list4[:], offs2)
+        nc.sync.dma_start(words4[:], tab2[0, 0:WORD_BYTES].rearrange("(p w) -> p w", p=P).bitcast(I32))
+        nc.sync.dma_start(list8[:], offs)
+
         nc.vector.memset(rows8[:], 0)
         nc.vector.memset(rows4[0:first4, :], 0)
+        nc.vector.memset(u_raw[:, 0, 0, 0:8], 0.0)
+        nc.vector.memset(words8[0][:, 0:8], 0)
+        nc.vector.memset(w_words[:, 0, 0:8], 0)
         nc.vector.memset(w_scales[:], 0)
+        nc.vector.memset(bias[:], 0.0)
         nc.vector.memset(plane4[:], 0)
         nc.vector.memset(warm[:], 0.0)
         nc.scalar.activation(warm_out[:], warm[:], GELU)
 
-        nc.sync.dma_start(list8[:], offs)
-        for q in range(QUADS):
+        for q in (0, 2, 1, 3):
             nc.sync.dma_start(rows8[QUAD * q : QUAD * q + LIVE, :, :], tab_scales[LIVE * q : LIVE * (q + 1)])
-        nc.sync.dma_start(words4[:], tab2[0, 0:WORD_BYTES].rearrange("(p w) -> p w", p=P).bitcast(I32))
         nc.sync.dma_start(u_raw[:], u.rearrange("(a p i) n -> p a i n", p=P, i=PACK))
         nc.sync.dma_start(words8[0][:], tab[0, 0:WORD_BYTES].rearrange("(p w) -> p w", p=P).bitcast(I32))
         nc.scalar.dma_start(w_words[:], w4_words.rearrange("a p n -> p a n").bitcast(I32))
@@ -92,16 +101,21 @@ def tile_list_tab48_gelu_kernel(tc, tab, w4_words, w4_scales, tab2, u, b, offs, 
             for q in range(QUADS):
                 row = first4 + LIVE * (QUADS * h + q)
                 nc.sync.dma_start(plane4[QUAD * q : QUAD * q + LIVE, h, :], got_rows4[row : row + LIVE, :].bitcast(I32))
-        for a in range(PASSES):
-            nc.vector.tensor_copy(plane8[:, a, :], rows8[:, a, :].bitcast(U8).indirect(list8[:]))
 
         nc.scalar.copy(u_bf[:], u_raw[:].rearrange("p a i n -> p a n i"))
         nc.sync.dma_start(words8[1][:], tab[1, 0:WORD_BYTES].rearrange("(p w) -> p w", p=P).bitcast(I32))
-        nc.vector.tensor_copy(got4[:], words4[:].bitcast(U32).indirect(list4[:]))
+
+        for c0, c1 in HALVES:
+            nc.vector.tensor_copy(got4[:, c0:c1], words4[:].bitcast(U32).indirect(list4[:, c0 // STRIPE : c1 // STRIPE]))
+        for c0, c1 in HALVES:
+            nc.vector.tensor_copy(
+                parted4[:, :, c0:c1], got4[:, c0:c1].bitcast(U16).rearrange("p (j h) -> p h j", h=PASSES)
+            )
+        nc.vector.tensor_copy(plane8[0][:], rows8[:, 0, :].bitcast(U8).indirect(list8[:]))
         nc.vector.quantize_mx(
             out=u_codes[:].bitcast(FP8X4), scales=u_scales[:], in_=u_bf[:].rearrange("p a n i -> p (a n i)")
         )
-        nc.vector.tensor_copy(parted4[:], got4[:].bitcast(U16).rearrange("p (j h) -> p h j", h=PASSES))
+        nc.vector.tensor_copy(plane8[1][:], rows8[:, 1, :].bitcast(U8).indirect(list8[:]))
         for g, (lo, hi) in enumerate(GROUPS):
             for h in range(PASSES):
                 nc.tensor.matmul_mx(
@@ -121,7 +135,7 @@ def tile_list_tab48_gelu_kernel(tc, tab, w4_words, w4_scales, tab2, u, b, offs, 
                 lhsT=w_words[:, a, :].bitcast(FP4X4),
                 lhsT_scale=w_scales[:, a, :].bitcast(U8),
                 rhs=got8[a][:, lo:hi].bitcast(FP8X4),
-                rhs_scale=plane8[:, a, lo:hi],
+                rhs_scale=plane8[a][:, lo:hi],
                 start=False,
                 stop=(a == PASSES - 1),
             )

@@ -24,9 +24,9 @@ LIVE = 4
 STRIPE = 16
 WORD_BYTES = P * PACK * T
 
-GROUPS = [(0, 512), (512, 640), (640, 768), (768, 896), (896, 1024)]
+GROUPS = [(lo, lo + 128) for lo in range(0, S, 128)]
 HALVES = [(0, 512), (512, 1024)]
-GATHERS8 = [(0, 0, 512), (1, 0, 512), (0, 512, 1024), (1, 512, 768), (1, 768, 1024)]
+GATHERS8 = [(0, 0, 512), (0, 512, 1024), (1, 0, 256), (1, 256, 512), (1, 512, 768), (1, 768, 1024)]
 STORE_FROM = {512: 0, 768: 512, 896: 768}
 
 

@@ -34,31 +34,32 @@ def tile_list_tab48_gelu_kernel(tc, tab, w4_words, w4_scales, tab2, u, b, offs, 
     nc = tc.nc
     with ExitStack() as ctx:
         keep = ctx.enter_context(tc.tile_pool(name="keep", bufs=1))
+        reused = ctx.enter_context(tc.tile_pool(name="reused", bufs=1))
         psum = ctx.enter_context(tc.psum_pool(name="psum", bufs=1))
 
         list8 = keep.tile([P, S // STRIPE], U16, name="list8")
         list4 = keep.tile([P, S // STRIPE], U16, name="list4")
-        rows4 = keep.tile([P, T // 4], I32, name="rows4", align_bytes=64)
-        rows8 = keep.tile([P, PASSES, T // 4], I32, name="rows8", align_bytes=64)
-        words4 = keep.tile([P, T], I32, name="words4", tag="after_words4", align_bytes=64)
-        u_raw = keep.tile([P, PASSES, PACK, M], F32, name="u_raw", tag="shared", align_bytes=64)
+        at_plane = 4 * T
+        at_u = at_plane - 1024
+        at_rows4 = 8 * T + S
+        rows4 = reused.tile([P, T // 4], I32, name="rows4", align_bytes=64, offset=at_rows4)
+        w_words = reused.tile([P, PASSES, 2 * M // 4], I32, name="w_words", align_bytes=64, offset=at_rows4)
+        w_scales = reused.tile([P, PASSES, M // 4], I32, name="w_scales", align_bytes=64, offset=at_rows4 + 512)
+        bias = reused.tile([P, 1], F32, name="bias", align_bytes=64, offset=at_rows4 + 768)
+        u_raw = reused.tile([P, PASSES, PACK, M], F32, name="u_raw", align_bytes=64, offset=at_u)
         words8 = [
-            keep.tile([P, T], I32, name="words8_0", align_bytes=64),
-            keep.tile([P, T], I32, name="words8_1", tag="shared", align_bytes=64),
+            reused.tile([P, T], I32, name=f"words8_{a}", align_bytes=64, offset=(4 * T + S) * a) for a in range(PASSES)
         ]
-        u_bf = keep.tile([P, PASSES, M, PACK], BF16, name="u_bf", tag="after_u_bf", align_bytes=64)
+        words4 = keep.tile([P, T], I32, name="words4", align_bytes=64)
+        rows8 = keep.tile([P, PASSES, T // 4], I32, name="rows8", align_bytes=64)
+        u_bf = keep.tile([P, PASSES, M, PACK], BF16, name="u_bf", align_bytes=64)
         u_codes = keep.tile([P, PASSES * M], U32, name="u_codes", align_bytes=64)
         u_scales = keep.tile([P, PASSES * M], U8, name="u_scales", align_bytes=64)
-        w_words = keep.tile([P, PASSES, 2 * M // 4], I32, name="w_words", align_bytes=64)
-        w_scales = keep.tile([P, PASSES, M // 4], I32, name="w_scales", align_bytes=64)
-        bias = keep.tile([P, 1], F32, name="bias")
-        warm = keep.tile([P, 1], F32, name="warm")
-        warm_out = keep.tile([P, 1], F32, name="warm_out")
         got_rows4 = keep.tile([P, S], U8, name="got_rows4", align_bytes=64)
         plane4 = keep.tile([P, PASSES, S // 4], I32, name="plane4", align_bytes=64)
         plane8 = [
-            keep.tile([P, S], U8, name="plane8_0", tag="after_words4", align_bytes=64),
-            keep.tile([P, S], U8, name="plane8_1", tag="after_u_bf", align_bytes=64),
+            keep.tile([P, S], U8, name="plane8_0", align_bytes=64),
+            reused.tile([P, S], U8, name="plane8_1", align_bytes=64, offset=at_plane),
         ]
         got4 = keep.tile([P, S], U32, name="got4", align_bytes=64)
         parted4 = keep.tile([P, PASSES, S], U16, name="parted4", align_bytes=64)
@@ -75,38 +76,31 @@ def tile_list_tab48_gelu_kernel(tc, tab, w4_words, w4_scales, tab2, u, b, offs, 
         nc.sync.dma_start(list4[:], offs2)
         nc.sync.dma_start(words4[:], tab2[0, 0:WORD_BYTES].rearrange("(p w) -> p w", p=P).bitcast(I32))
         nc.sync.dma_start(list8[:], offs)
+        nc.sync.dma_start(u_raw[:], u.rearrange("(a p i) n -> p a i n", p=P, i=PACK))
 
         nc.vector.memset(rows8[:], 0)
         nc.vector.memset(rows4[0:first4, :], 0)
-        nc.vector.memset(u_raw[:, 0, 0, 0:8], 0.0)
-        nc.vector.memset(words8[0][:, 0:8], 0)
-        nc.vector.memset(w_words[:, 0, 0:8], 0)
-        nc.vector.memset(w_scales[:], 0)
-        nc.vector.memset(bias[:], 0.0)
-        nc.vector.memset(plane4[:], 0)
-        nc.vector.memset(warm[:], 0.0)
-        nc.scalar.activation(warm_out[:], warm[:], GELU)
 
         for q in (0, 2, 1, 3):
             nc.sync.dma_start(rows8[QUAD * q : QUAD * q + LIVE, :, :], tab_scales[LIVE * q : LIVE * (q + 1)])
-        nc.sync.dma_start(u_raw[:], u.rearrange("(a p i) n -> p a i n", p=P, i=PACK))
-        nc.sync.dma_start(words8[0][:], tab[0, 0:WORD_BYTES].rearrange("(p w) -> p w", p=P).bitcast(I32))
-        nc.scalar.dma_start(w_words[:], w4_words.rearrange("a p n -> p a n").bitcast(I32))
-        for q in range(QUADS):
-            nc.scalar.dma_start(w_scales[QUAD * q : QUAD * q + LIVE, :, :], w4_scale_rows[LIVE * q : LIVE * (q + 1)])
-        nc.scalar.dma_start(bias[:], b.rearrange("(p o) -> p o", o=1))
 
         nc.vector.tensor_copy(got_rows4[:], rows4[:].bitcast(U8).indirect(list4[:]))
+
+        nc.scalar.copy(u_bf[:], u_raw[:].rearrange("p a i n -> p a n i"))
+        for c0, c1 in HALVES:
+            nc.vector.tensor_copy(got4[:, c0:c1], words4[:].bitcast(U32).indirect(list4[:, c0 // STRIPE : c1 // STRIPE]))
+        nc.sync.dma_start(words8[0][:], tab[0, 0:WORD_BYTES].rearrange("(p w) -> p w", p=P).bitcast(I32))
+        nc.sync.dma_start(words8[1][:], tab[1, 0:WORD_BYTES].rearrange("(p w) -> p w", p=P).bitcast(I32))
         for h in range(PASSES):
             for q in range(QUADS):
                 row = first4 + LIVE * (QUADS * h + q)
                 nc.sync.dma_start(plane4[QUAD * q : QUAD * q + LIVE, h, :], got_rows4[row : row + LIVE, :].bitcast(I32))
+        nc.sync.dma_start(w_words[:], w4_words.rearrange("a p n -> p a n").bitcast(I32))
+        for q in range(QUADS):
+            nc.sync.dma_start(w_scales[QUAD * q : QUAD * q + LIVE, :, :], w4_scale_rows[LIVE * q : LIVE * (q + 1)])
+        nc.sync.dma_start(bias[:], b.rearrange("(p o) -> p o", o=1))
 
-        nc.scalar.copy(u_bf[:], u_raw[:].rearrange("p a i n -> p a n i"))
-        nc.sync.dma_start(words8[1][:], tab[1, 0:WORD_BYTES].rearrange("(p w) -> p w", p=P).bitcast(I32))
 
-        for c0, c1 in HALVES:
-            nc.vector.tensor_copy(got4[:, c0:c1], words4[:].bitcast(U32).indirect(list4[:, c0 // STRIPE : c1 // STRIPE]))
         for c0, c1 in HALVES:
             nc.vector.tensor_copy(
                 parted4[:, :, c0:c1], got4[:, c0:c1].bitcast(U16).rearrange("p (j h) -> p h j", h=PASSES)

@@ -39,16 +39,17 @@ def tile_list_tab48_gelu_kernel(tc, tab, w4_words, w4_scales, tab2, u, b, offs, 
 
         list8 = keep.tile([P, S // STRIPE], U16, name="list8")
         list4 = keep.tile([P, S // STRIPE], U16, name="list4")
+        at_u = 4 * T - 512
         at_plane = 4 * T
-        at_u = at_plane - 1024
-        at_rows4 = 8 * T + S
-        rows4 = reused.tile([P, T // 4], I32, name="rows4", align_bytes=64, offset=at_rows4)
-        w_words = reused.tile([P, PASSES, 2 * M // 4], I32, name="w_words", align_bytes=64, offset=at_rows4)
-        w_scales = reused.tile([P, PASSES, M // 4], I32, name="w_scales", align_bytes=64, offset=at_rows4 + 512)
-        bias = reused.tile([P, 1], F32, name="bias", align_bytes=64, offset=at_rows4 + 768)
+        at_w = at_plane + PASSES * S
+        rows4 = keep.tile([P, T // 4], I32, name="rows4", align_bytes=64)
         u_raw = reused.tile([P, PASSES, PACK, M], F32, name="u_raw", align_bytes=64, offset=at_u)
+        w_words = reused.tile([P, PASSES, 2 * M // 4], I32, name="w_words", align_bytes=64, offset=at_w)
+        w_scales = reused.tile([P, PASSES, M // 4], I32, name="w_scales", align_bytes=64, offset=at_w + 512)
+        bias = reused.tile([P, 1], F32, name="bias", align_bytes=64, offset=at_w + 768)
         words8 = [
-            reused.tile([P, T], I32, name=f"words8_{a}", align_bytes=64, offset=(4 * T + S) * a) for a in range(PASSES)
+            reused.tile([P, T], I32, name="words8_0", align_bytes=64, offset=0),
+            reused.tile([P, T], I32, name="words8_1", align_bytes=64, offset=at_w + 832),
         ]
         words4 = keep.tile([P, T], I32, name="words4", align_bytes=64)
         rows8 = keep.tile([P, PASSES, T // 4], I32, name="rows8", align_bytes=64)
@@ -58,8 +59,7 @@ def tile_list_tab48_gelu_kernel(tc, tab, w4_words, w4_scales, tab2, u, b, offs, 
         got_rows4 = keep.tile([P, S], U8, name="got_rows4", align_bytes=64)
         plane4 = keep.tile([P, PASSES, S // 4], I32, name="plane4", align_bytes=64)
         plane8 = [
-            keep.tile([P, S], U8, name="plane8_0", align_bytes=64),
-            reused.tile([P, S], U8, name="plane8_1", align_bytes=64, offset=at_plane),
+            reused.tile([P, S], U8, name=f"plane8_{a}", align_bytes=64, offset=at_plane + a * S) for a in range(PASSES)
         ]
         got4 = keep.tile([P, S], U32, name="got4", align_bytes=64)
         parted4 = keep.tile([P, PASSES, S], U16, name="parted4", align_bytes=64)
@@ -85,20 +85,20 @@ def tile_list_tab48_gelu_kernel(tc, tab, w4_words, w4_scales, tab2, u, b, offs, 
             nc.sync.dma_start(rows8[QUAD * q : QUAD * q + LIVE, :, :], tab_scales[LIVE * q : LIVE * (q + 1)])
 
         nc.vector.tensor_copy(got_rows4[:], rows4[:].bitcast(U8).indirect(list4[:]))
+        for h in range(PASSES):
+            for q in range(QUADS):
+                row = first4 + LIVE * (QUADS * h + q)
+                nc.sync.dma_start(plane4[QUAD * q : QUAD * q + LIVE, h, :], got_rows4[row : row + LIVE, :].bitcast(I32))
 
         nc.scalar.copy(u_bf[:], u_raw[:].rearrange("p a i n -> p a n i"))
         for c0, c1 in HALVES:
             nc.vector.tensor_copy(got4[:, c0:c1], words4[:].bitcast(U32).indirect(list4[:, c0 // STRIPE : c1 // STRIPE]))
         nc.sync.dma_start(words8[0][:], tab[0, 0:WORD_BYTES].rearrange("(p w) -> p w", p=P).bitcast(I32))
-        nc.sync.dma_start(words8[1][:], tab[1, 0:WORD_BYTES].rearrange("(p w) -> p w", p=P).bitcast(I32))
-        for h in range(PASSES):
-            for q in range(QUADS):
-                row = first4 + LIVE * (QUADS * h + q)
-                nc.sync.dma_start(plane4[QUAD * q : QUAD * q + LIVE, h, :], got_rows4[row : row + LIVE, :].bitcast(I32))
         nc.sync.dma_start(w_words[:], w4_words.rearrange("a p n -> p a n").bitcast(I32))
         for q in range(QUADS):
             nc.sync.dma_start(w_scales[QUAD * q : QUAD * q + LIVE, :, :], w4_scale_rows[LIVE * q : LIVE * (q + 1)])
         nc.sync.dma_start(bias[:], b.rearrange("(p o) -> p o", o=1))
+        nc.sync.dma_start(words8[1][:], tab[1, 0:WORD_BYTES].rearrange("(p w) -> p w", p=P).bitcast(I32))
 
 
         for c0, c1 in HALVES:

@@ -39,27 +39,30 @@ def tile_list_tab48_gelu_kernel(tc, tab, w4_words, w4_scales, tab2, u, b, offs, 
 
         list8 = keep.tile([P, S // STRIPE], U16, name="list8")
         list4 = keep.tile([P, S // STRIPE], U16, name="list4")
-        at_u = 4 * T - 512
-        at_plane = 4 * T
-        at_w = at_plane + PASSES * S
-        rows4 = keep.tile([P, T // 4], I32, name="rows4", align_bytes=64)
+        at_u = 0
+        at_w = 0
+        rows4 = reused.tile([P, T // 4], I32, name="rows4", align_bytes=64, offset=at_u)
+        words4 = keep.tile([P, T], I32, name="words4", align_bytes=64)
         u_raw = reused.tile([P, PASSES, PACK, M], F32, name="u_raw", align_bytes=64, offset=at_u)
         w_words = reused.tile([P, PASSES, 2 * M // 4], I32, name="w_words", align_bytes=64, offset=at_w)
         w_scales = reused.tile([P, PASSES, M // 4], I32, name="w_scales", align_bytes=64, offset=at_w + 512)
         bias = reused.tile([P, 1], F32, name="bias", align_bytes=64, offset=at_w + 768)
-        words8 = [
-            reused.tile([P, T], I32, name="words8_0", align_bytes=64, offset=0),
-            reused.tile([P, T], I32, name="words8_1", align_bytes=64, offset=at_w + 832),
+        rows8 = [
+            keep.tile([P, T // 4], I32, name="rows8_0", tag="table8", align_bytes=64),
+            keep.tile([P, T // 4], I32, name="rows8_1", align_bytes=64),
         ]
-        words4 = keep.tile([P, T], I32, name="words4", align_bytes=64)
-        rows8 = keep.tile([P, PASSES, T // 4], I32, name="rows8", align_bytes=64)
+        words8 = [
+            keep.tile([P, T], I32, name="words8_0", tag="table8", align_bytes=64),
+            reused.tile([P, T], I32, name="words8_1", align_bytes=64, offset=at_w + 832 + S),
+        ]
         u_bf = keep.tile([P, PASSES, M, PACK], BF16, name="u_bf", align_bytes=64)
         u_codes = keep.tile([P, PASSES * M], U32, name="u_codes", align_bytes=64)
         u_scales = keep.tile([P, PASSES * M], U8, name="u_scales", align_bytes=64)
         got_rows4 = keep.tile([P, S], U8, name="got_rows4", align_bytes=64)
         plane4 = keep.tile([P, PASSES, S // 4], I32, name="plane4", align_bytes=64)
         plane8 = [
-            reused.tile([P, S], U8, name=f"plane8_{a}", align_bytes=64, offset=at_plane + a * S) for a in range(PASSES)
+            keep.tile([P, S], U8, name="plane8_0", align_bytes=64),
+            reused.tile([P, S], U8, name="plane8_1", align_bytes=64, offset=at_w + 832),
         ]
         got4 = keep.tile([P, S], U32, name="got4", align_bytes=64)
         parted4 = keep.tile([P, PASSES, S], U16, name="parted4", align_bytes=64)
@@ -74,23 +77,26 @@ def tile_list_tab48_gelu_kernel(tc, tab, w4_words, w4_scales, tab2, u, b, offs, 
 
         nc.sync.dma_start(rows4[first4:P, :], tab2_scales)
         nc.sync.dma_start(list4[:], offs2)
-        nc.sync.dma_start(words4[:], tab2[0, 0:WORD_BYTES].rearrange("(p w) -> p w", p=P).bitcast(I32))
         nc.sync.dma_start(list8[:], offs)
-        nc.sync.dma_start(u_raw[:], u.rearrange("(a p i) n -> p a i n", p=P, i=PACK))
+        nc.sync.dma_start(words4[:], tab2[0, 0:WORD_BYTES].rearrange("(p w) -> p w", p=P).bitcast(I32))
 
-        nc.vector.memset(rows8[:], 0)
+        nc.vector.memset(rows8[0][:], 0)
         nc.vector.memset(rows4[0:first4, :], 0)
+        nc.vector.memset(rows8[1][:], 0)
 
-        for q in (0, 2, 1, 3):
-            nc.sync.dma_start(rows8[QUAD * q : QUAD * q + LIVE, :, :], tab_scales[LIVE * q : LIVE * (q + 1)])
+        for a in range(PASSES):
+            for q in (0, 2, 1, 3):
+                (nc.scalar, nc.sync)[a].dma_start(rows8[a][QUAD * q : QUAD * q + LIVE, :], tab_scales[LIVE * q : LIVE * (q + 1), a, :])
 
         nc.vector.tensor_copy(got_rows4[:], rows4[:].bitcast(U8).indirect(list4[:]))
+        nc.sync.dma_start(u_raw[:], u.rearrange("(a p i) n -> p a i n", p=P, i=PACK))
         for h in range(PASSES):
             for q in range(QUADS):
                 row = first4 + LIVE * (QUADS * h + q)
                 nc.sync.dma_start(plane4[QUAD * q : QUAD * q + LIVE, h, :], got_rows4[row : row + LIVE, :].bitcast(I32))
 
         nc.scalar.copy(u_bf[:], u_raw[:].rearrange("p a i n -> p a n i"))
+        nc.vector.tensor_copy(plane8[0][:], rows8[0][:].bitcast(U8).indirect(list8[:]))
         for c0, c1 in HALVES:
             nc.vector.tensor_copy(got4[:, c0:c1], words4[:].bitcast(U32).indirect(list4[:, c0 // STRIPE : c1 // STRIPE]))
         nc.sync.dma_start(words8[0][:], tab[0, 0:WORD_BYTES].rearrange("(p w) -> p w", p=P).bitcast(I32))
@@ -105,11 +111,10 @@ def tile_list_tab48_gelu_kernel(tc, tab, w4_words, w4_scales, tab2, u, b, offs, 
             nc.vector.tensor_copy(
                 parted4[:, :, c0:c1], got4[:, c0:c1].bitcast(U16).rearrange("p (j h) -> p h j", h=PASSES)
             )
-        nc.vector.tensor_copy(plane8[0][:], rows8[:, 0, :].bitcast(U8).indirect(list8[:]))
         nc.vector.quantize_mx(
             out=u_codes[:].bitcast(FP8X4), scales=u_scales[:], in_=u_bf[:].rearrange("p a n i -> p (a n i)")
         )
-        nc.vector.tensor_copy(plane8[1][:], rows8[:, 1, :].bitcast(U8).indirect(list8[:]))
+        nc.vector.tensor_copy(plane8[1][:], rows8[1][:].bitcast(U8).indirect(list8[:]))
         for g, (lo, hi) in enumerate(GROUPS):
             for h in range(PASSES):
                 nc.tensor.matmul_mx(

@@ -41,12 +41,12 @@ def tile_list_tab48_gelu_kernel(tc, tab, w4_words, w4_scales, tab2, u, b, offs, 
         list4 = keep.tile([P, S // STRIPE], U16, name="list4")
         at_u = 0
         at_w = 0
-        rows4 = reused.tile([P, T // 4], I32, name="rows4", align_bytes=64, offset=at_u)
+        rows4 = keep.tile([P, T // 4], I32, name="rows4", align_bytes=64)
         words4 = keep.tile([P, T], I32, name="words4", align_bytes=64)
         u_raw = reused.tile([P, PASSES, PACK, M], F32, name="u_raw", align_bytes=64, offset=at_u)
-        w_words = reused.tile([P, PASSES, 2 * M // 4], I32, name="w_words", align_bytes=64, offset=at_w)
+        w_words = keep.tile([P, PASSES, 2 * M // 4], I32, name="w_words", align_bytes=64)
         w_scales = reused.tile([P, PASSES, M // 4], I32, name="w_scales", align_bytes=64, offset=at_w + 512)
-        bias = reused.tile([P, 1], F32, name="bias", align_bytes=64, offset=at_w + 768)
+        bias = keep.tile([P, 1], F32, name="bias")
         rows8 = [
             keep.tile([P, T // 4], I32, name="rows8_0", tag="table8", align_bytes=64),
             keep.tile([P, T // 4], I32, name="rows8_1", align_bytes=64),
@@ -78,18 +78,23 @@ def tile_list_tab48_gelu_kernel(tc, tab, w4_words, w4_scales, tab2, u, b, offs, 
         nc.sync.dma_start(rows4[first4:P, :], tab2_scales)
         nc.sync.dma_start(list4[:], offs2)
         nc.sync.dma_start(list8[:], offs)
-        nc.sync.dma_start(words4[:], tab2[0, 0:WORD_BYTES].rearrange("(p w) -> p w", p=P).bitcast(I32))
+        nc.sync.dma_start(w_words[:], w4_words.rearrange("a p n -> p a n").bitcast(I32))
+        nc.sync.dma_start(bias[:], b.rearrange("(p o) -> p o", o=1))
 
         nc.vector.memset(rows8[0][:], 0)
         nc.vector.memset(rows4[0:first4, :], 0)
         nc.vector.memset(rows8[1][:], 0)
 
-        for a in range(PASSES):
+        def load_rows8(a):
             for q in (0, 2, 1, 3):
-                (nc.scalar, nc.sync)[a].dma_start(rows8[a][QUAD * q : QUAD * q + LIVE, :], tab_scales[LIVE * q : LIVE * (q + 1), a, :])
+                nc.sync.dma_start(rows8[a][QUAD * q : QUAD * q + LIVE, :], tab_scales[LIVE * q : LIVE * (q + 1), a, :])
+
+        load_rows8(0)
+        nc.sync.dma_start(words4[:], tab2[0, 0:WORD_BYTES].rearrange("(p w) -> p w", p=P).bitcast(I32))
+        nc.sync.dma_start(u_raw[:], u.rearrange("(a p i) n -> p a i n", p=P, i=PACK))
+        load_rows8(1)
 
         nc.vector.tensor_copy(got_rows4[:], rows4[:].bitcast(U8).indirect(list4[:]))
-        nc.sync.dma_start(u_raw[:], u.rearrange("(a p i) n -> p a i n", p=P, i=PACK))
         for h in range(PASSES):
             for q in range(QUADS):
                 row = first4 + LIVE * (QUADS * h + q)
@@ -100,10 +105,8 @@ def tile_list_tab48_gelu_kernel(tc, tab, w4_words, w4_scales, tab2, u, b, offs, 
         for c0, c1 in HALVES:
             nc.vector.tensor_copy(got4[:, c0:c1], words4[:].bitcast(U32).indirect(list4[:, c0 // STRIPE : c1 // STRIPE]))
         nc.sync.dma_start(words8[0][:], tab[0, 0:WORD_BYTES].rearrange("(p w) -> p w", p=P).bitcast(I32))
-        nc.sync.dma_start(w_words[:], w4_words.rearrange("a p n -> p a n").bitcast(I32))
         for q in range(QUADS):
             nc.sync.dma_start(w_scales[QUAD * q : QUAD * q + LIVE, :, :], w4_scale_rows[LIVE * q : LIVE * (q + 1)])
-        nc.sync.dma_start(bias[:], b.rearrange("(p o) -> p o", o=1))
         nc.sync.dma_start(words8[1][:], tab[1, 0:WORD_BYTES].rearrange("(p w) -> p w", p=P).bitcast(I32))
 
 

@@ -25,8 +25,7 @@ STRIPE = 16
 WORD_BYTES = P * PACK * T
 
 GROUPS = [(lo, lo + 128) for lo in range(0, S, 128)]
-HALVES = [(0, 512), (512, 1024)]
-GATHERS8 = [(0, 0, 512), (0, 512, 1024), (1, 0, 256), (1, 256, 512), (1, 512, 768), (1, 768, 1024)]
+GATHERS8 = [(0, 0, 1024), (1, 0, 512), (1, 512, 768), (1, 768, 1024)]
 STORE_FROM = {512: 0, 768: 512, 896: 768}
 
 
@@ -39,13 +38,13 @@ def tile_list_tab48_gelu_kernel(tc, tab, w4_words, w4_scales, tab2, u, b, offs, 
 
         list8 = keep.tile([P, S // STRIPE], U16, name="list8")
         list4 = keep.tile([P, S // STRIPE], U16, name="list4")
-        at_u = 0
-        at_w = 0
+        at_w = 2 * PASSES * S
+        at_u = at_w - 1024
         rows4 = keep.tile([P, T // 4], I32, name="rows4", align_bytes=64)
         words4 = keep.tile([P, T], I32, name="words4", align_bytes=64)
         u_raw = reused.tile([P, PASSES, PACK, M], F32, name="u_raw", align_bytes=64, offset=at_u)
         w_words = keep.tile([P, PASSES, 2 * M // 4], I32, name="w_words", align_bytes=64)
-        w_scales = reused.tile([P, PASSES, M // 4], I32, name="w_scales", align_bytes=64, offset=at_w + 512)
+        w_scales = reused.tile([P, PASSES, M // 4], I32, name="w_scales", align_bytes=64, offset=at_w)
         bias = keep.tile([P, 1], F32, name="bias")
         rows8 = [
             keep.tile([P, T // 4], I32, name="rows8_0", tag="table8", align_bytes=64),
@@ -53,7 +52,7 @@ def tile_list_tab48_gelu_kernel(tc, tab, w4_words, w4_scales, tab2, u, b, offs, 
         ]
         words8 = [
             keep.tile([P, T], I32, name="words8_0", tag="table8", align_bytes=64),
-            reused.tile([P, T], I32, name="words8_1", align_bytes=64, offset=at_w + 832 + S),
+            reused.tile([P, T], I32, name="words8_1", align_bytes=64, offset=at_w + 256),
         ]
         u_bf = keep.tile([P, PASSES, M, PACK], BF16, name="u_bf", align_bytes=64)
         u_codes = keep.tile([P, PASSES * M], U32, name="u_codes", align_bytes=64)
@@ -62,10 +61,10 @@ def tile_list_tab48_gelu_kernel(tc, tab, w4_words, w4_scales, tab2, u, b, offs, 
         plane4 = keep.tile([P, PASSES, S // 4], I32, name="plane4", align_bytes=64)
         plane8 = [
             keep.tile([P, S], U8, name="plane8_0", align_bytes=64),
-            reused.tile([P, S], U8, name="plane8_1", align_bytes=64, offset=at_w + 832),
+            keep.tile([P, S], U8, name="plane8_1", align_bytes=64),
         ]
         got4 = keep.tile([P, S], U32, name="got4", align_bytes=64)
-        parted4 = keep.tile([P, PASSES, S], U16, name="parted4", align_bytes=64)
+        parted4 = reused.tile([P, PASSES, S], U16, name="parted4", align_bytes=64, offset=0)
         got8 = [keep.tile([P, S], U32, name=f"got8_{a}", align_bytes=64) for a in range(PASSES)]
         result = keep.tile([P, S], F32, name="result", align_bytes=64)
         acc = [psum.tile([P, hi - lo], F32, name=f"acc{g}") for g, (lo, hi) in enumerate(GROUPS)]
@@ -91,8 +90,8 @@ def tile_list_tab48_gelu_kernel(tc, tab, w4_words, w4_scales, tab2, u, b, offs, 
 
         load_rows8(0)
         nc.sync.dma_start(words4[:], tab2[0, 0:WORD_BYTES].rearrange("(p w) -> p w", p=P).bitcast(I32))
-        nc.sync.dma_start(u_raw[:], u.rearrange("(a p i) n -> p a i n", p=P, i=PACK))
         load_rows8(1)
+        nc.sync.dma_start(u_raw[:], u.rearrange("(a p i) n -> p a i n", p=P, i=PACK))
 
         nc.vector.tensor_copy(got_rows4[:], rows4[:].bitcast(U8).indirect(list4[:]))
         for h in range(PASSES):
@@ -102,22 +101,18 @@ def tile_list_tab48_gelu_kernel(tc, tab, w4_words, w4_scales, tab2, u, b, offs, 
 
         nc.scalar.copy(u_bf[:], u_raw[:].rearrange("p a i n -> p a n i"))
         nc.vector.tensor_copy(plane8[0][:], rows8[0][:].bitcast(U8).indirect(list8[:]))
-        for c0, c1 in HALVES:
-            nc.vector.tensor_copy(got4[:, c0:c1], words4[:].bitcast(U32).indirect(list4[:, c0 // STRIPE : c1 // STRIPE]))
+        nc.vector.tensor_copy(got4[:], words4[:].bitcast(U32).indirect(list4[:]))
+        nc.vector.tensor_copy(plane8[1][:], rows8[1][:].bitcast(U8).indirect(list8[:]))
         nc.sync.dma_start(words8[0][:], tab[0, 0:WORD_BYTES].rearrange("(p w) -> p w", p=P).bitcast(I32))
         for q in range(QUADS):
             nc.sync.dma_start(w_scales[QUAD * q : QUAD * q + LIVE, :, :], w4_scale_rows[LIVE * q : LIVE * (q + 1)])
         nc.sync.dma_start(words8[1][:], tab[1, 0:WORD_BYTES].rearrange("(p w) -> p w", p=P).bitcast(I32))
 
 
-        for c0, c1 in HALVES:
-            nc.vector.tensor_copy(
-                parted4[:, :, c0:c1], got4[:, c0:c1].bitcast(U16).rearrange("p (j h) -> p h j", h=PASSES)
-            )
+        nc.vector.tensor_copy(parted4[:], got4[:].bitcast(U16).rearrange("p (j h) -> p h j", h=PASSES))
         nc.vector.quantize_mx(
             out=u_codes[:].bitcast(FP8X4), scales=u_scales[:], in_=u_bf[:].rearrange("p a n i -> p (a n i)")
         )
-        nc.vector.tensor_copy(plane8[1][:], rows8[1][:].bitcast(U8).indirect(list8[:]))
         for g, (lo, hi) in enumerate(GROUPS):
             for h in range(PASSES):
                 nc.tensor.matmul_mx(

@@ -43,16 +43,16 @@ def tile_list_tab48_gelu_kernel(tc, tab, w4_words, w4_scales, tab2, u, b, offs, 
         rows4 = keep.tile([P, T // 4], I32, name="rows4", align_bytes=64)
         words4 = keep.tile([P, T], I32, name="words4", align_bytes=64)
         u_raw = reused.tile([P, PASSES, PACK, M], F32, name="u_raw", align_bytes=64, offset=at_u)
-        w_words = keep.tile([P, PASSES, 2 * M // 4], I32, name="w_words", align_bytes=64)
+        w_words = reused.tile([P, PASSES, 2 * M // 4], I32, name="w_words", align_bytes=64, offset=at_w + 320)
         w_scales = reused.tile([P, PASSES, M // 4], I32, name="w_scales", align_bytes=64, offset=at_w)
-        bias = keep.tile([P, 1], F32, name="bias")
+        bias = reused.tile([P, 1], F32, name="bias", align_bytes=64, offset=at_w + 256)
         rows8 = [
             keep.tile([P, T // 4], I32, name="rows8_0", tag="table8", align_bytes=64),
             keep.tile([P, T // 4], I32, name="rows8_1", align_bytes=64),
         ]
         words8 = [
             keep.tile([P, T], I32, name="words8_0", tag="table8", align_bytes=64),
-            reused.tile([P, T], I32, name="words8_1", align_bytes=64, offset=at_w + 256),
+            reused.tile([P, T], I32, name="words8_1", align_bytes=64, offset=at_w + 832),
         ]
         u_bf = keep.tile([P, PASSES, M, PACK], BF16, name="u_bf", align_bytes=64)
         u_codes = keep.tile([P, PASSES * M], U32, name="u_codes", align_bytes=64)
@@ -77,8 +77,6 @@ def tile_list_tab48_gelu_kernel(tc, tab, w4_words, w4_scales, tab2, u, b, offs, 
         nc.sync.dma_start(rows4[first4:P, :], tab2_scales)
         nc.sync.dma_start(list4[:], offs2)
         nc.sync.dma_start(list8[:], offs)
-        nc.sync.dma_start(w_words[:], w4_words.rearrange("a p n -> p a n").bitcast(I32))
-        nc.sync.dma_start(bias[:], b.rearrange("(p o) -> p o", o=1))
 
         nc.vector.memset(rows8[0][:], 0)
         nc.vector.memset(rows4[0:first4, :], 0)
@@ -107,7 +105,8 @@ def tile_list_tab48_gelu_kernel(tc, tab, w4_words, w4_scales, tab2, u, b, offs, 
         for q in range(QUADS):
             nc.sync.dma_start(w_scales[QUAD * q : QUAD * q + LIVE, :, :], w4_scale_rows[LIVE * q : LIVE * (q + 1)])
         nc.sync.dma_start(words8[1][:], tab[1, 0:WORD_BYTES].rearrange("(p w) -> p w", p=P).bitcast(I32))
-
+        nc.sync.dma_start(w_words[:], w4_words.rearrange("a p n -> p a n").bitcast(I32))
+        nc.sync.dma_start(bias[:], b.rearrange("(p o) -> p o", o=1))
 
         nc.vector.tensor_copy(parted4[:], got4[:].bitcast(U16).rearrange("p (j h) -> p h j", h=PASSES))
         nc.vector.quantize_mx(

@@ -38,35 +38,36 @@ def tile_list_tab48_gelu_kernel(tc, tab, w4_words, w4_scales, tab2, u, b, offs, 
 
         list8 = keep.tile([P, S // STRIPE], U16, name="list8")
         list4 = keep.tile([P, S // STRIPE], U16, name="list4")
+        far = 32 * 1024
         at_w = 2 * PASSES * S
         at_u = at_w - 1024
-        rows4 = keep.tile([P, T // 4], I32, name="rows4", align_bytes=64)
-        words4 = keep.tile([P, T], I32, name="words4", align_bytes=64)
+        rows4 = reused.tile([P, T // 4], I32, name="rows4", align_bytes=64, offset=far)
+        words4 = reused.tile([P, T], I32, name="words4", align_bytes=64, offset=2 * far)
         u_raw = reused.tile([P, PASSES, PACK, M], F32, name="u_raw", align_bytes=64, offset=at_u)
         w_words = reused.tile([P, PASSES, 2 * M // 4], I32, name="w_words", align_bytes=64, offset=at_w + 320)
         w_scales = reused.tile([P, PASSES, M // 4], I32, name="w_scales", align_bytes=64, offset=at_w)
         bias = reused.tile([P, 1], F32, name="bias", align_bytes=64, offset=at_w + 256)
         rows8 = [
-            keep.tile([P, T // 4], I32, name="rows8_0", tag="table8", align_bytes=64),
-            keep.tile([P, T // 4], I32, name="rows8_1", align_bytes=64),
+            reused.tile([P, T // 4], I32, name="rows8_0", align_bytes=64, offset=3 * far),
+            reused.tile([P, T // 4], I32, name="rows8_1", align_bytes=64, offset=4 * far),
         ]
         words8 = [
-            keep.tile([P, T], I32, name="words8_0", tag="table8", align_bytes=64),
+            reused.tile([P, T], I32, name="words8_0", align_bytes=64, offset=3 * far),
             reused.tile([P, T], I32, name="words8_1", align_bytes=64, offset=at_w + 832),
         ]
         u_bf = keep.tile([P, PASSES, M, PACK], BF16, name="u_bf", align_bytes=64)
         u_codes = keep.tile([P, PASSES * M], U32, name="u_codes", align_bytes=64)
         u_scales = keep.tile([P, PASSES * M], U8, name="u_scales", align_bytes=64)
-        got_rows4 = keep.tile([P, S], U8, name="got_rows4", align_bytes=64)
-        plane4 = keep.tile([P, PASSES, S // 4], I32, name="plane4", align_bytes=64)
+        got_rows4 = reused.tile([P, S], U8, name="got_rows4", align_bytes=64, offset=5 * far)
+        plane4 = reused.tile([P, PASSES, S // 4], I32, name="plane4", align_bytes=64, offset=5 * far + S)
         plane8 = [
-            keep.tile([P, S], U8, name="plane8_0", align_bytes=64),
-            keep.tile([P, S], U8, name="plane8_1", align_bytes=64),
+            reused.tile([P, S], U8, name="plane8_0", align_bytes=64, offset=6 * far),
+            reused.tile([P, S], U8, name="plane8_1", align_bytes=64, offset=6 * far + S),
         ]
-        got4 = keep.tile([P, S], U32, name="got4", align_bytes=64)
+        got4 = reused.tile([P, S], U32, name="got4", align_bytes=64, offset=6 * far + 2 * S)
         parted4 = reused.tile([P, PASSES, S], U16, name="parted4", align_bytes=64, offset=0)
-        got8 = [keep.tile([P, S], U32, name=f"got8_{a}", align_bytes=64) for a in range(PASSES)]
-        result = keep.tile([P, S], F32, name="result", align_bytes=64)
+        got8 = [reused.tile([P, S], U32, name=f"got8_{a}", align_bytes=64, offset=6 * far + (6 + 4 * a) * S) for a in range(PASSES)]
+        result = reused.tile([P, S], F32, name="result", align_bytes=64, offset=far + T)
         acc = [psum.tile([P, hi - lo], F32, name=f"acc{g}") for g, (lo, hi) in enumerate(GROUPS)]
 
         first4 = P - PASSES * QUADS * LIVE

@@ -52,8 +52,8 @@ def tile_list_tab48_gelu_kernel(tc, tab, w4_words, w4_scales, tab2, u, b, offs, 
             reused.tile([P, T // 4], I32, name="rows8_1", align_bytes=64, offset=4 * far),
         ]
         words8 = [
-            reused.tile([P, T], I32, name="words8_0", align_bytes=64, offset=3 * far),
-            reused.tile([P, T], I32, name="words8_1", align_bytes=64, offset=at_w + 832),
+            reused.tile([P, T], I32, name="words8_0", align_bytes=64, offset=far + 4 * T),
+            reused.tile([P, T], I32, name="words8_1", align_bytes=64, offset=4 * T),
         ]
         u_bf = keep.tile([P, PASSES, M, PACK], BF16, name="u_bf", align_bytes=64)
         u_codes = keep.tile([P, PASSES * M], U32, name="u_codes", align_bytes=64)
@@ -66,7 +66,7 @@ def tile_list_tab48_gelu_kernel(tc, tab, w4_words, w4_scales, tab2, u, b, offs, 
         ]
         got4 = reused.tile([P, S], U32, name="got4", align_bytes=64, offset=6 * far + 2 * S)
         parted4 = reused.tile([P, PASSES, S], U16, name="parted4", align_bytes=64, offset=0)
-        got8 = [reused.tile([P, S], U32, name=f"got8_{a}", align_bytes=64, offset=6 * far + (6 + 4 * a) * S) for a in range(PASSES)]
+        got8 = [reused.tile([P, S], U32, name=f"got8_{a}", align_bytes=64, offset=6 * far + (2 + 4 * a) * S) for a in range(PASSES)]
         result = reused.tile([P, S], F32, name="result", align_bytes=64, offset=far + T)
         acc = [psum.tile([P, hi - lo], F32, name=f"acc{g}") for g, (lo, hi) in enumerate(GROUPS)]
 
@@ -91,6 +91,8 @@ def tile_list_tab48_gelu_kernel(tc, tab, w4_words, w4_scales, tab2, u, b, offs, 
         nc.sync.dma_start(words4[:], tab2[0, 0:WORD_BYTES].rearrange("(p w) -> p w", p=P).bitcast(I32))
         load_rows8(1)
         nc.sync.dma_start(u_raw[:], u.rearrange("(a p i) n -> p a i n", p=P, i=PACK))
+        for a in range(PASSES):
+            nc.sync.dma_start(words8[a][:], tab[a, 0:WORD_BYTES].rearrange("(p w) -> p w", p=P).bitcast(I32))
 
         nc.vector.tensor_copy(got_rows4[:], rows4[:].bitcast(U8).indirect(list4[:]))
         for h in range(PASSES):
@@ -102,10 +104,8 @@ def tile_list_tab48_gelu_kernel(tc, tab, w4_words, w4_scales, tab2, u, b, offs, 
         nc.vector.tensor_copy(plane8[0][:], rows8[0][:].bitcast(U8).indirect(list8[:]))
         nc.vector.tensor_copy(got4[:], words4[:].bitcast(U32).indirect(list4[:]))
         nc.vector.tensor_copy(plane8[1][:], rows8[1][:].bitcast(U8).indirect(list8[:]))
-        nc.sync.dma_start(words8[0][:], tab[0, 0:WORD_BYTES].rearrange("(p w) -> p w", p=P).bitcast(I32))
         for q in range(QUADS):
             nc.sync.dma_start(w_scales[QUAD * q : QUAD * q + LIVE, :, :], w4_scale_rows[LIVE * q : LIVE * (q + 1)])
-        nc.sync.dma_start(words8[1][:], tab[1, 0:WORD_BYTES].rearrange("(p w) -> p w", p=P).bitcast(I32))
         nc.sync.dma_start(w_words[:], w4_words.rearrange("a p n -> p a n").bitcast(I32))
         nc.sync.dma_start(bias[:], b.rearrange("(p o) -> p o", o=1))
 

@@ -84,8 +84,8 @@ def tile_list_tab48_gelu_kernel(tc, tab, w4_words, w4_scales, tab2, u, b, offs, 
         nc.vector.memset(rows8[1][:], 0)
 
         def load_rows8(a):
-            for q in (0, 2, 1, 3):
-                nc.sync.dma_start(rows8[a][QUAD * q : QUAD * q + LIVE, :], tab_scales[LIVE * q : LIVE * (q + 1), a, :])
+            for r in range(LIVE):
+                nc.sync.dma_start(rows8[a][r:P:QUAD, :], tab_scales[r : QUADS * LIVE : LIVE, a, :])
 
         load_rows8(0)
         nc.sync.dma_start(words4[:], tab2[0, 0:WORD_BYTES].rearrange("(p w) -> p w", p=P).bitcast(I32))
@@ -96,16 +96,16 @@ def tile_list_tab48_gelu_kernel(tc, tab, w4_words, w4_scales, tab2, u, b, offs, 
 
         nc.vector.tensor_copy(got_rows4[:], rows4[:].bitcast(U8).indirect(list4[:]))
         for h in range(PASSES):
-            for q in range(QUADS):
-                row = first4 + LIVE * (QUADS * h + q)
-                nc.sync.dma_start(plane4[QUAD * q : QUAD * q + LIVE, h, :], got_rows4[row : row + LIVE, :].bitcast(I32))
+            for r in range(LIVE):
+                row = first4 + QUADS * LIVE * h
+                nc.sync.dma_start(plane4[r:P:QUAD, h, :], got_rows4[row + r : row + QUADS * LIVE : LIVE, :].bitcast(I32))
 
         nc.scalar.copy(u_bf[:], u_raw[:].rearrange("p a i n -> p a n i"))
         nc.vector.tensor_copy(plane8[0][:], rows8[0][:].bitcast(U8).indirect(list8[:]))
         nc.vector.tensor_copy(got4[:], words4[:].bitcast(U32).indirect(list4[:]))
         nc.vector.tensor_copy(plane8[1][:], rows8[1][:].bitcast(U8).indirect(list8[:]))
-        for q in range(QUADS):
-            nc.sync.dma_start(w_scales[QUAD * q : QUAD * q + LIVE, :, :], w4_scale_rows[LIVE * q : LIVE * (q + 1)])
+        for r in range(LIVE):
+            nc.sync.dma_start(w_scales[r:P:QUAD, :, :], w4_scale_rows[r : QUADS * LIVE : LIVE])
         nc.sync.dma_start(w_words[:], w4_words.rearrange("a p n -> p a n").bitcast(I32))
         nc.sync.dma_start(bias[:], b.rearrange("(p o) -> p o", o=1))
 

@@ -51,10 +51,7 @@ def tile_list_tab48_gelu_kernel(tc, tab, w4_words, w4_scales, tab2, u, b, offs, 
             reused.tile([P, T // 4], I32, name="rows8_0", align_bytes=64, offset=3 * far),
             reused.tile([P, T // 4], I32, name="rows8_1", align_bytes=64, offset=4 * far),
         ]
-        words8 = [
-            reused.tile([P, T], I32, name="words8_0", align_bytes=64, offset=far + 4 * T),
-            reused.tile([P, T], I32, name="words8_1", align_bytes=64, offset=4 * T),
-        ]
+        words8 = reused.tile([P, PASSES, T], I32, name="words8", align_bytes=64, offset=far + 4 * T)
         u_bf = keep.tile([P, PASSES, M, PACK], BF16, name="u_bf", align_bytes=64)
         u_codes = keep.tile([P, PASSES * M], U32, name="u_codes", align_bytes=64)
         u_scales = keep.tile([P, PASSES * M], U8, name="u_scales", align_bytes=64)
@@ -91,8 +88,7 @@ def tile_list_tab48_gelu_kernel(tc, tab, w4_words, w4_scales, tab2, u, b, offs, 
         nc.sync.dma_start(words4[:], tab2[0, 0:WORD_BYTES].rearrange("(p w) -> p w", p=P).bitcast(I32))
         load_rows8(1)
         nc.sync.dma_start(u_raw[:], u.rearrange("(a p i) n -> p a i n", p=P, i=PACK))
-        for a in range(PASSES):
-            nc.sync.dma_start(words8[a][:], tab[a, 0:WORD_BYTES].rearrange("(p w) -> p w", p=P).bitcast(I32))
+        nc.sync.dma_start(words8[:], tab[:, 0:WORD_BYTES].rearrange("a (p w) -> p a w", p=P).bitcast(I32))
 
         nc.vector.tensor_copy(got_rows4[:], rows4[:].bitcast(U8).indirect(list4[:]))
         for h in range(PASSES):
@@ -139,7 +135,7 @@ def tile_list_tab48_gelu_kernel(tc, tab, w4_words, w4_scales, tab2, u, b, offs, 
 
         for a, c0, c1 in GATHERS8:
             nc.vector.tensor_copy(
-                got8[a][:, c0:c1], words8[a][:].bitcast(U32).indirect(list8[:, c0 // STRIPE : c1 // STRIPE])
+                got8[a][:, c0:c1], words8[:, a, :].bitcast(U32).indirect(list8[:, c0 // STRIPE : c1 // STRIPE])
             )
             for g, (lo, hi) in enumerate(GROUPS):
                 if c0 <= lo < c1:

@@ -143,6 +143,6 @@ def tile_list_tab48_gelu_kernel(tc, tab, w4_words, w4_scales, tab2, u, b, offs, 
                     if a == PASSES - 1:
                         nc.scalar.activation(result[:, lo:hi], acc[g][:], GELU, bias=bias[:])
                         if hi == S:
-                            nc.scalar.dma_start(out[:, lo:hi], result[:, lo:hi])
+                            nc.sync.dma_start(out[:, lo:hi], result[:, lo:hi])
                         elif hi in STORE_FROM:
                             nc.sync.dma_start(out[:, STORE_FROM[hi] : hi], result[:, STORE_FROM[hi] : hi])

@@ -25,7 +25,7 @@ STRIPE = 16
 WORD_BYTES = P * PACK * T
 
 GROUPS = [(lo, lo + 128) for lo in range(0, S, 128)]
-GATHERS8 = [(0, 0, 1024), (1, 0, 512), (1, 512, 768), (1, 768, 1024)]
+GATHERS8 = [(0, 0, 512), (1, 0, 768), (0, 512, 1024), (1, 768, 1024)]
 STORE_FROM = {512: 0, 768: 512, 896: 768}
 
 
@@ -121,7 +121,7 @@ def tile_list_tab48_gelu_kernel(tc, tab, w4_words, w4_scales, tab2, u, b, offs, 
                     stop=False,
                 )
 
-        def table8_pass(a, g):
+        def table8_pass(a, g, last):
             lo, hi = GROUPS[g]
             nc.tensor.matmul_mx(
                 out=acc[g][:],
@@ -130,17 +130,20 @@ def tile_list_tab48_gelu_kernel(tc, tab, w4_words, w4_scales, tab2, u, b, offs, 
                 rhs=got8[a][:, lo:hi].bitcast(FP8X4),
                 rhs_scale=plane8[a][:, lo:hi],
                 start=False,
-                stop=(a == PASSES - 1),
+                stop=last,
             )
 
+        done = set()
         for a, c0, c1 in GATHERS8:
             nc.vector.tensor_copy(
                 got8[a][:, c0:c1], words8[:, a, :].bitcast(U32).indirect(list8[:, c0 // STRIPE : c1 // STRIPE])
             )
             for g, (lo, hi) in enumerate(GROUPS):
                 if c0 <= lo < c1:
-                    table8_pass(a, g)
-                    if a == PASSES - 1:
+                    last = g in done
+                    done.add(g)
+                    table8_pass(a, g, last)
+                    if last:
                         nc.scalar.activation(result[:, lo:hi], acc[g][:], GELU, bias=bias[:])
                         if hi == S:
                             nc.sync.dma_start(out[:, lo:hi], result[:, lo:hi])

@@ -62,8 +62,12 @@ def tile_list_tab48_gelu_kernel(tc, tab, w4_words, w4_scales, tab2, u, b, offs, 
             reused.tile([P, S], U8, name="plane8_1", align_bytes=64, offset=6 * far + S),
         ]
         got4 = reused.tile([P, S], U32, name="got4", align_bytes=64, offset=6 * far + 2 * S)
-        parted4 = reused.tile([P, PASSES, S], U16, name="parted4", align_bytes=64, offset=0)
-        got8 = [reused.tile([P, S], U32, name=f"got8_{a}", align_bytes=64, offset=6 * far + (2 + 4 * a) * S) for a in range(PASSES)]
+        parted4 = reused.tile([P, PASSES, S - M], U16, name="parted4", align_bytes=64, offset=0)
+        got8 = [
+            reused.tile([P, c1 - c0], U32, name=f"got8_{a}_{c0}", align_bytes=64, offset=6 * far + (6 + 4 * a) * S + 4 * c0)
+            for a, c0, c1 in GATHERS8
+        ]
+        parted_last = reused.tile([P, PASSES, M], U16, name="parted_last", align_bytes=64, offset=6 * far + 6 * S)
         result = reused.tile([P, S], F32, name="result", align_bytes=64, offset=far + T)
         acc = [psum.tile([P, hi - lo], F32, name=f"acc{g}") for g, (lo, hi) in enumerate(GROUPS)]
 
@@ -105,44 +109,53 @@ def tile_list_tab48_gelu_kernel(tc, tab, w4_words, w4_scales, tab2, u, b, offs, 
         nc.sync.dma_start(w_words[:], w4_words.rearrange("a p n -> p a n").bitcast(I32))
         nc.sync.dma_start(bias[:], b.rearrange("(p o) -> p o", o=1))
 
-        nc.vector.tensor_copy(parted4[:], got4[:].bitcast(U16).rearrange("p (j h) -> p h j", h=PASSES))
+        halves4 = got4[:].bitcast(U16).rearrange("p (j h) -> p h j", h=PASSES)
+        nc.vector.tensor_copy(parted4[:], halves4[:, :, 0 : S - M])
         nc.vector.quantize_mx(
             out=u_codes[:].bitcast(FP8X4), scales=u_scales[:], in_=u_bf[:].rearrange("p a n i -> p (a n i)")
         )
-        for g, (lo, hi) in enumerate(GROUPS):
+
+        def table4_passes(g, words, first):
+            lo, hi = GROUPS[g]
             for h in range(PASSES):
                 nc.tensor.matmul_mx(
                     out=acc[g][:],
                     lhsT=u_codes[:, h * M : (h + 1) * M].bitcast(FP8X4),
                     lhsT_scale=u_scales[:, h * M : (h + 1) * M],
-                    rhs=parted4[:, h, lo:hi].bitcast(FP4X4),
+                    rhs=words[:, h, :].bitcast(FP4X4),
                     rhs_scale=plane4[:, h, :].bitcast(U8)[:, lo:hi],
-                    start=(h == 0),
-                    stop=False,
+                    start=(first and h == 0),
+                    stop=(not first and h == PASSES - 1),
                 )
 
-        def table8_pass(a, g, last):
+        for g, (lo, hi) in enumerate(GROUPS[:-1]):
+            table4_passes(g, parted4[:, :, lo:hi], True)
+
+        def table8_pass(a, g, words, first, last):
             lo, hi = GROUPS[g]
             nc.tensor.matmul_mx(
                 out=acc[g][:],
                 lhsT=w_words[:, a, :].bitcast(FP4X4),
                 lhsT_scale=w_scales[:, a, :].bitcast(U8),
-                rhs=got8[a][:, lo:hi].bitcast(FP8X4),
+                rhs=words.bitcast(FP8X4),
                 rhs_scale=plane8[a][:, lo:hi],
-                start=False,
+                start=first,
                 stop=last,
             )
 
         done = set()
-        for a, c0, c1 in GATHERS8:
+        for got, (a, c0, c1) in zip(got8, GATHERS8):
             nc.vector.tensor_copy(
-                got8[a][:, c0:c1], words8[:, a, :].bitcast(U32).indirect(list8[:, c0 // STRIPE : c1 // STRIPE])
+                got[:], words8[:, a, :].bitcast(U32).indirect(list8[:, c0 // STRIPE : c1 // STRIPE])
             )
             for g, (lo, hi) in enumerate(GROUPS):
                 if c0 <= lo < c1:
                     last = g in done
                     done.add(g)
-                    table8_pass(a, g, last)
+                    table8_pass(a, g, got[:, lo - c0 : hi - c0], hi == S and not last, hi < S and last)
+                    if last and hi == S:
+                        nc.vector.tensor_copy(parted_last[:], halves4[:, :, lo:hi])
+                        table4_passes(g, parted_last, False)
                     if last:
                         nc.scalar.activation(result[:, lo:hi], acc[g][:], GELU, bias=bias[:])
                         if hi == S:

@@ -44,9 +44,9 @@ def tile_list_tab48_gelu_kernel(tc, tab, w4_words, w4_scales, tab2, u, b, offs, 
         rows4 = reused.tile([P, T // 4], I32, name="rows4", align_bytes=64, offset=far)
         words4 = reused.tile([P, T], I32, name="words4", align_bytes=64, offset=2 * far)
         u_raw = reused.tile([P, PASSES, PACK, M], F32, name="u_raw", align_bytes=64, offset=at_u)
-        w_words = reused.tile([P, PASSES, 2 * M // 4], I32, name="w_words", align_bytes=64, offset=at_w + 320)
-        w_scales = reused.tile([P, PASSES, M // 4], I32, name="w_scales", align_bytes=64, offset=at_w)
-        bias = reused.tile([P, 1], F32, name="bias", align_bytes=64, offset=at_w + 256)
+        w_words = reused.tile([P, PASSES, 2 * M // 4], I32, name="w_words", align_bytes=64, offset=far)
+        w_scales = reused.tile([P, PASSES, M // 4], I32, name="w_scales", align_bytes=64, offset=5 * far)
+        bias = reused.tile([P, 1], F32, name="bias", align_bytes=64, offset=far + 512)
         rows8 = [
             reused.tile([P, T // 4], I32, name="rows8_0", align_bytes=64, offset=3 * far),
             reused.tile([P, T // 4], I32, name="rows8_1", align_bytes=64, offset=4 * far),
@@ -95,6 +95,8 @@ def tile_list_tab48_gelu_kernel(tc, tab, w4_words, w4_scales, tab2, u, b, offs, 
         nc.sync.dma_start(words8[:], tab[:, 0:WORD_BYTES].rearrange("a (p w) -> p a w", p=P).bitcast(I32))
 
         nc.vector.tensor_copy(got_rows4[:], rows4[:].bitcast(U8).indirect(list4[:]))
+        nc.sync.dma_start(w_words[:], w4_words.rearrange("a p n -> p a n").bitcast(I32))
+        nc.sync.dma_start(bias[:], b.rearrange("(p o) -> p o", o=1))
         for h in range(PASSES):
             for r in range(LIVE):
                 row = first4 + QUADS * LIVE * h
@@ -106,8 +108,6 @@ def tile_list_tab48_gelu_kernel(tc, tab, w4_words, w4_scales, tab2, u, b, offs, 
         nc.vector.tensor_copy(plane8[1][:], rows8[1][:].bitcast(U8).indirect(list8[:]))
         for r in range(LIVE):
             nc.sync.dma_start(w_scales[r:P:QUAD, :, :], w4_scale_rows[r : QUADS * LIVE : LIVE])
-        nc.sync.dma_start(w_words[:], w4_words.rearrange("a p n -> p a n").bitcast(I32))
-        nc.sync.dma_start(bias[:], b.rearrange("(p o) -> p o", o=1))
 
         halves4 = got4[:].bitcast(U16).rearrange("p (j h) -> p h j", h=PASSES)
         nc.vector.tensor_copy(parted4[:], halves4[:, :, 0 : S - M])

@@ -21,12 +21,14 @@ PASSES = 2
 QUADS = 4
 QUAD = 32
 LIVE = 4
+ROWS = QUADS * LIVE
 STRIPE = 16
 WORD_BYTES = P * PACK * T
+TAB2, TAB = 0, 1
 
 GROUPS = [(lo, lo + 128) for lo in range(0, S, 128)]
-GATHERS8 = [(0, 0, 512), (1, 0, 768), (0, 512, 1024), (1, 768, 1024)]
-STORE_FROM = {512: 0, 768: 512, 896: 768}
+GATHERS8 = [(0, 0, 512), (1, 0, 768), (0, 512, 1024), (1, 768, 896), (1, 896, 1024)]
+STORE_FROM = {256: 0, 512: 256, 768: 512, 896: 768, 1024: 896}
 
 
 def tile_list_tab48_gelu_kernel(tc, tab, w4_words, w4_scales, tab2, u, b, offs, offs2, out):
@@ -38,127 +40,98 @@ def tile_list_tab48_gelu_kernel(tc, tab, w4_words, w4_scales, tab2, u, b, offs, 
 
         list8 = keep.tile([P, S // STRIPE], U16, name="list8")
         list4 = keep.tile([P, S // STRIPE], U16, name="list4")
-        far = 32 * 1024
-        at_w = 2 * PASSES * S
-        at_u = at_w - 1024
-        rows4 = reused.tile([P, T // 4], I32, name="rows4", align_bytes=64, offset=far)
-        words4 = reused.tile([P, T], I32, name="words4", align_bytes=64, offset=2 * far)
-        u_raw = reused.tile([P, PASSES, PACK, M], F32, name="u_raw", align_bytes=64, offset=at_u)
-        w_words = reused.tile([P, PASSES, 2 * M // 4], I32, name="w_words", align_bytes=64, offset=far)
-        w_scales = reused.tile([P, PASSES, M // 4], I32, name="w_scales", align_bytes=64, offset=5 * far)
-        bias = reused.tile([P, 1], F32, name="bias", align_bytes=64, offset=far + 512)
-        rows8 = [
-            reused.tile([P, T // 4], I32, name="rows8_0", align_bytes=64, offset=3 * far),
-            reused.tile([P, T // 4], I32, name="rows8_1", align_bytes=64, offset=4 * far),
-        ]
-        words8 = reused.tile([P, PASSES, T], I32, name="words8", align_bytes=64, offset=far + 4 * T)
+        rows4 = keep.tile([P, T // 4], I32, name="rows4", align_bytes=64)
+        rows8 = keep.tile([P, T // 4], I32, name="rows8", align_bytes=64)
+        words4 = keep.tile([P, T], I32, name="words4", align_bytes=64)
+        words8 = [keep.tile([P, T], I32, name=f"words8_{a}", align_bytes=64) for a in range(PASSES)]
+        w_words = keep.tile([P, PASSES, 2 * M // 4], I32, name="w_words", align_bytes=64)
+        w_scales = keep.tile([P, PASSES, M // 4], I32, name="w_scales", align_bytes=64)
+        bias = keep.tile([P, 1], F32, name="bias", align_bytes=64)
         u_bf = keep.tile([P, PASSES, M, PACK], BF16, name="u_bf", align_bytes=64)
         u_codes = keep.tile([P, PASSES * M], U32, name="u_codes", align_bytes=64)
         u_scales = keep.tile([P, PASSES * M], U8, name="u_scales", align_bytes=64)
-        got_rows4 = reused.tile([P, S], U8, name="got_rows4", align_bytes=64, offset=5 * far)
-        plane4 = reused.tile([P, PASSES, S // 4], I32, name="plane4", align_bytes=64, offset=5 * far + S)
-        plane8 = [
-            reused.tile([P, S], U8, name="plane8_0", align_bytes=64, offset=6 * far),
-            reused.tile([P, S], U8, name="plane8_1", align_bytes=64, offset=6 * far + S),
-        ]
-        got4 = reused.tile([P, S], U32, name="got4", align_bytes=64, offset=6 * far + 2 * S)
-        parted4 = reused.tile([P, PASSES, S - M], U16, name="parted4", align_bytes=64, offset=0)
+        planes = keep.tile([P, PASSES, 2, S // 4], I32, name="planes", align_bytes=64)
+        got4 = keep.tile([P, S], U32, name="got4", align_bytes=64)
+        result = keep.tile([P, S], F32, name="result", align_bytes=64)
+
+        u_raw = reused.tile([P, PASSES, PACK, M], F32, name="u_raw", align_bytes=64, offset=0)
+        parted4 = reused.tile([P, PASSES, S], U16, name="parted4", align_bytes=64, offset=0)
+        got_rows = reused.tile([P, 2, S], U8, name="got_rows", align_bytes=64, offset=4 * S + 1536)
+        at_got8 = [8 * S, 10 * S, 4 * S, 6 * S, 6 * S + 512]
         got8 = [
-            reused.tile([P, c1 - c0], U32, name=f"got8_{a}_{c0}", align_bytes=64, offset=6 * far + (6 + 4 * a) * S + 4 * c0)
-            for a, c0, c1 in GATHERS8
+            reused.tile([P, c1 - c0], U32, name=f"got8_{a}_{c0}", align_bytes=64, offset=at)
+            for (a, c0, c1), at in zip(GATHERS8, at_got8)
         ]
-        parted_last = reused.tile([P, PASSES, M], U16, name="parted_last", align_bytes=64, offset=6 * far + 6 * S)
-        result = reused.tile([P, S], F32, name="result", align_bytes=64, offset=far + T)
         acc = [psum.tile([P, hi - lo], F32, name=f"acc{g}") for g, (lo, hi) in enumerate(GROUPS)]
 
-        first4 = P - PASSES * QUADS * LIVE
-        tab_scales = tab[:, WORD_BYTES:].rearrange("a (q t) -> q a t", t=T).bitcast(I32)
+        first = P - PASSES * ROWS
+        tab_scales = tab[:, WORD_BYTES:].rearrange("a (q t) -> a q t", t=T).bitcast(I32)
         tab2_scales = tab2[0, WORD_BYTES:].rearrange("(q t) -> q t", t=T).bitcast(I32)
         w4_scale_rows = w4_scales.rearrange("a q n -> q a n").bitcast(I32)
 
-        nc.sync.dma_start(rows4[first4:P, :], tab2_scales)
+        nc.sync.dma_start(rows4[first:P, :], tab2_scales)
         nc.sync.dma_start(list4[:], offs2)
         nc.sync.dma_start(list8[:], offs)
-
-        nc.vector.memset(rows8[0][:], 0)
-        nc.vector.memset(rows4[0:first4, :], 0)
-        nc.vector.memset(rows8[1][:], 0)
-
-        def load_rows8(a):
-            for r in range(LIVE):
-                nc.sync.dma_start(rows8[a][r:P:QUAD, :], tab_scales[r : QUADS * LIVE : LIVE, a, :])
-
-        load_rows8(0)
+        for a in range(PASSES):
+            nc.sync.dma_start(rows8[first + ROWS * a : first + ROWS * (a + 1), :], tab_scales[a])
         nc.sync.dma_start(words4[:], tab2[0, 0:WORD_BYTES].rearrange("(p w) -> p w", p=P).bitcast(I32))
-        load_rows8(1)
         nc.sync.dma_start(u_raw[:], u.rearrange("(a p i) n -> p a i n", p=P, i=PACK))
-        nc.sync.dma_start(words8[:], tab[:, 0:WORD_BYTES].rearrange("a (p w) -> p a w", p=P).bitcast(I32))
-
-        nc.vector.tensor_copy(got_rows4[:], rows4[:].bitcast(U8).indirect(list4[:]))
+        nc.sync.dma_start(words8[0][:], tab[0, 0:WORD_BYTES].rearrange("(p w) -> p w", p=P).bitcast(I32))
         nc.sync.dma_start(w_words[:], w4_words.rearrange("a p n -> p a n").bitcast(I32))
         nc.sync.dma_start(bias[:], b.rearrange("(p o) -> p o", o=1))
+        for r in range(LIVE):
+            nc.sync.dma_start(w_scales[r:P:QUAD, :, :], w4_scale_rows[r:ROWS:LIVE])
+        nc.sync.dma_start(words8[1][:], tab[1, 0:WORD_BYTES].rearrange("(p w) -> p w", p=P).bitcast(I32))
+
+        nc.vector.memset(rows4[0:first, :], 0)
+        nc.vector.memset(rows8[0:first, :], 0)
+
+        nc.vector.tensor_copy(got_rows[:, TAB2, :], rows4[:].bitcast(U8).indirect(list4[:]))
+        nc.vector.tensor_copy(got_rows[:, TAB, :], rows8[:].bitcast(U8).indirect(list8[:]))
+        got_rows_words = got_rows[:].rearrange("p t s -> p (t s)").bitcast(I32)
         for h in range(PASSES):
             for r in range(LIVE):
-                row = first4 + QUADS * LIVE * h
-                nc.sync.dma_start(plane4[r:P:QUAD, h, :], got_rows4[row + r : row + QUADS * LIVE : LIVE, :].bitcast(I32))
+                row = first + ROWS * h
+                nc.sync.dma_start(
+                    planes[r:P:QUAD, h, :, :].rearrange("p t s -> p (t s)"), got_rows_words[row + r : row + ROWS : LIVE, :]
+                )
 
         nc.scalar.copy(u_bf[:], u_raw[:].rearrange("p a i n -> p a n i"))
-        nc.vector.tensor_copy(plane8[0][:], rows8[0][:].bitcast(U8).indirect(list8[:]))
         nc.vector.tensor_copy(got4[:], words4[:].bitcast(U32).indirect(list4[:]))
-        nc.vector.tensor_copy(plane8[1][:], rows8[1][:].bitcast(U8).indirect(list8[:]))
-        for r in range(LIVE):
-            nc.sync.dma_start(w_scales[r:P:QUAD, :, :], w4_scale_rows[r : QUADS * LIVE : LIVE])
-
-        halves4 = got4[:].bitcast(U16).rearrange("p (j h) -> p h j", h=PASSES)
-        nc.vector.tensor_copy(parted4[:], halves4[:, :, 0 : S - M])
         nc.vector.quantize_mx(
             out=u_codes[:].bitcast(FP8X4), scales=u_scales[:], in_=u_bf[:].rearrange("p a n i -> p (a n i)")
         )
+        nc.vector.tensor_copy(parted4[:], got4[:].bitcast(U16).rearrange("p (j h) -> p h j", h=PASSES))
 
-        def table4_passes(g, words, first):
-            lo, hi = GROUPS[g]
-            for h in range(PASSES):
+        for h in range(PASSES):
+            for g, (lo, hi) in enumerate(GROUPS):
                 nc.tensor.matmul_mx(
                     out=acc[g][:],
                     lhsT=u_codes[:, h * M : (h + 1) * M].bitcast(FP8X4),
                     lhsT_scale=u_scales[:, h * M : (h + 1) * M],
-                    rhs=words[:, h, :].bitcast(FP4X4),
-                    rhs_scale=plane4[:, h, :].bitcast(U8)[:, lo:hi],
-                    start=(first and h == 0),
-                    stop=(not first and h == PASSES - 1),
+                    rhs=parted4[:, h, lo:hi].bitcast(FP4X4),
+                    rhs_scale=planes[:, h, TAB2, :].bitcast(U8)[:, lo:hi],
+                    start=(h == 0),
+                    stop=False,
                 )
 
-        for g, (lo, hi) in enumerate(GROUPS[:-1]):
-            table4_passes(g, parted4[:, :, lo:hi], True)
-
-        def table8_pass(a, g, words, first, last):
-            lo, hi = GROUPS[g]
-            nc.tensor.matmul_mx(
-                out=acc[g][:],
-                lhsT=w_words[:, a, :].bitcast(FP4X4),
-                lhsT_scale=w_scales[:, a, :].bitcast(U8),
-                rhs=words.bitcast(FP8X4),
-                rhs_scale=plane8[a][:, lo:hi],
-                start=first,
-                stop=last,
-            )
-
-        done = set()
+        opened = set()
         for got, (a, c0, c1) in zip(got8, GATHERS8):
-            nc.vector.tensor_copy(
-                got[:], words8[:, a, :].bitcast(U32).indirect(list8[:, c0 // STRIPE : c1 // STRIPE])
-            )
+            nc.vector.tensor_copy(got[:], words8[a][:].bitcast(U32).indirect(list8[:, c0 // STRIPE : c1 // STRIPE]))
             for g, (lo, hi) in enumerate(GROUPS):
                 if c0 <= lo < c1:
-                    last = g in done
-                    done.add(g)
-                    table8_pass(a, g, got[:, lo - c0 : hi - c0], hi == S and not last, hi < S and last)
-                    if last and hi == S:
-                        nc.vector.tensor_copy(parted_last[:], halves4[:, :, lo:hi])
-                        table4_passes(g, parted_last, False)
+                    last = g in opened
+                    opened.add(g)
+                    nc.tensor.matmul_mx(
+                        out=acc[g][:],
+                        lhsT=w_words[:, a, :].bitcast(FP4X4),
+                        lhsT_scale=w_scales[:, a, :].bitcast(U8),
+                        rhs=got[:, lo - c0 : hi - c0].bitcast(FP8X4),
+                        rhs_scale=planes[:, a, TAB, :].bitcast(U8)[:, lo:hi],
+                        start=False,
+                        stop=last,
+                    )
                     if last:
                         nc.scalar.activation(result[:, lo:hi], acc[g][:], GELU, bias=bias[:])
-                        if hi == S:
-                            nc.sync.dma_start(out[:, lo:hi], result[:, lo:hi])
-                        elif hi in STORE_FROM:
+                        if hi in STORE_FROM:
                             nc.sync.dma_start(out[:, STORE_FROM[hi] : hi], result[:, STORE_FROM[hi] : hi])

@@ -41,21 +41,24 @@ def tile_list_tab48_gelu_kernel(tc, tab, w4_words, w4_scales, tab2, u, b, offs, 
         list8 = keep.tile([P, S // STRIPE], U16, name="list8")
         list4 = keep.tile([P, S // STRIPE], U16, name="list4")
         rows4 = keep.tile([P, T // 4], I32, name="rows4", align_bytes=64)
-        rows8 = keep.tile([P, T // 4], I32, name="rows8", align_bytes=64)
         words4 = keep.tile([P, T], I32, name="words4", align_bytes=64)
-        words8 = [keep.tile([P, T], I32, name=f"words8_{a}", align_bytes=64) for a in range(PASSES)]
         w_words = keep.tile([P, PASSES, 2 * M // 4], I32, name="w_words", align_bytes=64)
         w_scales = keep.tile([P, PASSES, M // 4], I32, name="w_scales", align_bytes=64)
         bias = keep.tile([P, 1], F32, name="bias", align_bytes=64)
         u_bf = keep.tile([P, PASSES, M, PACK], BF16, name="u_bf", align_bytes=64)
         u_codes = keep.tile([P, PASSES * M], U32, name="u_codes", align_bytes=64)
         u_scales = keep.tile([P, PASSES * M], U8, name="u_scales", align_bytes=64)
-        planes = keep.tile([P, PASSES, 2, S // 4], I32, name="planes", align_bytes=64)
+        planes = [keep.tile([P, 2, S // 4], I32, name=f"planes{h}", align_bytes=64) for h in range(PASSES)]
         got4 = keep.tile([P, S], U32, name="got4", align_bytes=64)
         result = keep.tile([P, S], F32, name="result", align_bytes=64)
 
         u_raw = reused.tile([P, PASSES, PACK, M], F32, name="u_raw", align_bytes=64, offset=0)
         parted4 = reused.tile([P, PASSES, S], U16, name="parted4", align_bytes=64, offset=0)
+        rows8 = reused.tile([P, T // 4], I32, name="rows8", align_bytes=64, offset=16 * S)
+        words8 = [
+            keep.tile([P, T], I32, name="words8_0", align_bytes=64),
+            reused.tile([P, T], I32, name="words8_1", align_bytes=64, offset=16 * S),
+        ]
         got_rows = reused.tile([P, 2, S], U8, name="got_rows", align_bytes=64, offset=4 * S + 1536)
         at_got8 = [8 * S, 10 * S, 4 * S, 6 * S, 6 * S + 512]
         got8 = [
@@ -76,12 +79,15 @@ def tile_list_tab48_gelu_kernel(tc, tab, w4_words, w4_scales, tab2, u, b, offs, 
             nc.sync.dma_start(rows8[first + ROWS * a : first + ROWS * (a + 1), :], tab_scales[a])
         nc.sync.dma_start(words4[:], tab2[0, 0:WORD_BYTES].rearrange("(p w) -> p w", p=P).bitcast(I32))
         nc.sync.dma_start(u_raw[:], u.rearrange("(a p i) n -> p a i n", p=P, i=PACK))
-        nc.sync.dma_start(words8[0][:], tab[0, 0:WORD_BYTES].rearrange("(p w) -> p w", p=P).bitcast(I32))
         nc.sync.dma_start(w_words[:], w4_words.rearrange("a p n -> p a n").bitcast(I32))
-        nc.sync.dma_start(bias[:], b.rearrange("(p o) -> p o", o=1))
         for r in range(LIVE):
             nc.sync.dma_start(w_scales[r:P:QUAD, :, :], w4_scale_rows[r:ROWS:LIVE])
-        nc.sync.dma_start(words8[1][:], tab[1, 0:WORD_BYTES].rearrange("(p w) -> p w", p=P).bitcast(I32))
+        nc.sync.dma_start(bias[:], b.rearrange("(p o) -> p o", o=1))
+
+        def load_words8(a):
+            nc.sync.dma_start(words8[a][:], tab[a, 0:WORD_BYTES].rearrange("(p w) -> p w", p=P).bitcast(I32))
+
+        load_words8(0)
 
         nc.vector.memset(rows4[0:first, :], 0)
         nc.vector.memset(rows8[0:first, :], 0)
@@ -89,12 +95,17 @@ def tile_list_tab48_gelu_kernel(tc, tab, w4_words, w4_scales, tab2, u, b, offs, 
         nc.vector.tensor_copy(got_rows[:, TAB2, :], rows4[:].bitcast(U8).indirect(list4[:]))
         nc.vector.tensor_copy(got_rows[:, TAB, :], rows8[:].bitcast(U8).indirect(list8[:]))
         got_rows_words = got_rows[:].rearrange("p t s -> p (t s)").bitcast(I32)
-        for h in range(PASSES):
+
+        def move_rows(h):
+            row = first + ROWS * h
             for r in range(LIVE):
-                row = first + ROWS * h
                 nc.sync.dma_start(
-                    planes[r:P:QUAD, h, :, :].rearrange("p t s -> p (t s)"), got_rows_words[row + r : row + ROWS : LIVE, :]
+                    planes[h][r:P:QUAD].rearrange("p t s -> p (t s)"), got_rows_words[row + r : row + ROWS : LIVE, :]
                 )
+
+        move_rows(0)
+        load_words8(1)
+        move_rows(1)
 
         nc.scalar.copy(u_bf[:], u_raw[:].rearrange("p a i n -> p a n i"))
         nc.vector.tensor_copy(got4[:], words4[:].bitcast(U32).indirect(list4[:]))
@@ -110,7 +121,7 @@ def tile_list_tab48_gelu_kernel(tc, tab, w4_words, w4_scales, tab2, u, b, offs, 
                     lhsT=u_codes[:, h * M : (h + 1) * M].bitcast(FP8X4),
                     lhsT_scale=u_scales[:, h * M : (h + 1) * M],
                     rhs=parted4[:, h, lo:hi].bitcast(FP4X4),
-                    rhs_scale=planes[:, h, TAB2, :].bitcast(U8)[:, lo:hi],
+                    rhs_scale=planes[h][:, TAB2, :].bitcast(U8)[:, lo:hi],
                     start=(h == 0),
                     stop=False,
                 )
@@ -127,7 +138,7 @@ def tile_list_tab48_gelu_kernel(tc, tab, w4_words, w4_scales, tab2, u, b, offs, 
                         lhsT=w_words[:, a, :].bitcast(FP4X4),
                         lhsT_scale=w_scales[:, a, :].bitcast(U8),
                         rhs=got[:, lo - c0 : hi - c0].bitcast(FP8X4),
-                        rhs_scale=planes[:, a, TAB, :].bitcast(U8)[:, lo:hi],
+                        rhs_scale=planes[a][:, TAB, :].bitcast(U8)[:, lo:hi],
                         start=False,
                         stop=last,
                     )

@@ -26,9 +26,8 @@ STRIPE = 16
 WORD_BYTES = P * PACK * T
 TAB2, TAB = 0, 1
 
-GROUPS = [(lo, lo + 128) for lo in range(0, S, 128)]
-GATHERS8 = [(0, 0, 512), (1, 0, 768), (0, 512, 1024), (1, 768, 896), (1, 896, 1024)]
-STORE_FROM = {256: 0, 512: 256, 768: 512, 896: 768, 1024: 896}
+GROUPS = [(0, 256), (256, 512), (512, 768), (768, 896), (896, 1024)]
+GATHERS8 = [(0, 0, 512), (0, 512, 1024)] + [(1, lo, hi) for lo, hi in GROUPS]
 
 
 def tile_list_tab48_gelu_kernel(tc, tab, w4_words, w4_scales, tab2, u, b, offs, offs2, out):
@@ -45,7 +44,7 @@ def tile_list_tab48_gelu_kernel(tc, tab, w4_words, w4_scales, tab2, u, b, offs, 
         w_words = keep.tile([P, PASSES, 2 * M // 4], I32, name="w_words", align_bytes=64)
         w_scales = keep.tile([P, PASSES, M // 4], I32, name="w_scales", align_bytes=64)
         bias = keep.tile([P, 1], F32, name="bias", align_bytes=64)
-        u_bf = keep.tile([P, PASSES, M, PACK], BF16, name="u_bf", align_bytes=64)
+        got_rows = keep.tile([P, 2, S], U8, name="got_rows", align_bytes=64)
         u_codes = keep.tile([P, PASSES * M], U32, name="u_codes", align_bytes=64)
         u_scales = keep.tile([P, PASSES * M], U8, name="u_scales", align_bytes=64)
         planes = [keep.tile([P, 2, S // 4], I32, name=f"planes{h}", align_bytes=64) for h in range(PASSES)]
@@ -59,11 +58,10 @@ def tile_list_tab48_gelu_kernel(tc, tab, w4_words, w4_scales, tab2, u, b, offs, 
             keep.tile([P, T], I32, name="words8_0", align_bytes=64),
             reused.tile([P, T], I32, name="words8_1", align_bytes=64, offset=16 * S),
         ]
-        got_rows = reused.tile([P, 2, S], U8, name="got_rows", align_bytes=64, offset=4 * S + 1536)
-        at_got8 = [8 * S, 10 * S, 4 * S, 6 * S, 6 * S + 512]
+        u_bf = reused.tile([P, PASSES, M, PACK], BF16, name="u_bf", align_bytes=64, offset=8 * S)
         got8 = [
-            reused.tile([P, c1 - c0], U32, name=f"got8_{a}_{c0}", align_bytes=64, offset=at)
-            for (a, c0, c1), at in zip(GATHERS8, at_got8)
+            reused.tile([P, S], U32, name="got8_0", align_bytes=64, offset=8 * S),
+            keep.tile([P, S], U32, name="got8_1", align_bytes=64),
         ]
         acc = [psum.tile([P, hi - lo], F32, name=f"acc{g}") for g, (lo, hi) in enumerate(GROUPS)]
 
@@ -114,7 +112,7 @@ def tile_list_tab48_gelu_kernel(tc, tab, w4_words, w4_scales, tab2, u, b, offs, 
         )
         nc.vector.tensor_copy(parted4[:], got4[:].bitcast(U16).rearrange("p (j h) -> p h j", h=PASSES))
 
-        for h in range(PASSES):
+        def table4_passes(h):
             for g, (lo, hi) in enumerate(GROUPS):
                 nc.tensor.matmul_mx(
                     out=acc[g][:],
@@ -126,23 +124,24 @@ def tile_list_tab48_gelu_kernel(tc, tab, w4_words, w4_scales, tab2, u, b, offs, 
                     stop=False,
                 )
 
-        opened = set()
-        for got, (a, c0, c1) in zip(got8, GATHERS8):
-            nc.vector.tensor_copy(got[:], words8[a][:].bitcast(U32).indirect(list8[:, c0 // STRIPE : c1 // STRIPE]))
+        table4_passes(0)
+
+        for a, c0, c1 in GATHERS8:
+            nc.vector.tensor_copy(got8[a][:, c0:c1], words8[a][:].bitcast(U32).indirect(list8[:, c0 // STRIPE : c1 // STRIPE]))
             for g, (lo, hi) in enumerate(GROUPS):
                 if c0 <= lo < c1:
-                    last = g in opened
-                    opened.add(g)
+                    last = a == PASSES - 1
                     nc.tensor.matmul_mx(
                         out=acc[g][:],
                         lhsT=w_words[:, a, :].bitcast(FP4X4),
                         lhsT_scale=w_scales[:, a, :].bitcast(U8),
-                        rhs=got[:, lo - c0 : hi - c0].bitcast(FP8X4),
+                        rhs=got8[a][:, lo:hi].bitcast(FP8X4),
                         rhs_scale=planes[a][:, TAB, :].bitcast(U8)[:, lo:hi],
                         start=False,
                         stop=last,
                     )
                     if last:
                         nc.scalar.activation(result[:, lo:hi], acc[g][:], GELU, bias=bias[:])
-                        if hi in STORE_FROM:
-                            nc.sync.dma_start(out[:, STORE_FROM[hi] : hi], result[:, STORE_FROM[hi] : hi])
+                        nc.sync.dma_start(out[:, lo:hi], result[:, lo:hi])
+            if c0 == 0 and a == 0:
+                table4_passes(1)

@@ -27,6 +27,7 @@ WORD_BYTES = P * PACK * T
 TAB2, TAB = 0, 1
 
 GROUPS = [(0, 256), (256, 512), (512, 768), (768, 896), (896, 1024)]
+STORES = [(lo, lo + 128) for lo in range(0, 512, 128)] + GROUPS[2:]
 GATHERS8 = [(0, 0, 512), (0, 512, 1024)] + [(1, lo, hi) for lo, hi in GROUPS]
 
 
@@ -83,7 +84,9 @@ def tile_list_tab48_gelu_kernel(tc, tab, w4_words, w4_scales, tab2, u, b, offs, 
         nc.sync.dma_start(bias[:], b.rearrange("(p o) -> p o", o=1))
 
         def load_words8(a):
-            nc.sync.dma_start(words8[a][:], tab[a, 0:WORD_BYTES].rearrange("(p w) -> p w", p=P).bitcast(I32))
+            words = tab[a, 0:WORD_BYTES].rearrange("(p w) -> p w", p=P).bitcast(I32)
+            for lo in range(0, T, T // 2):
+                nc.sync.dma_start(words8[a][:, lo : lo + T // 2], words[:, lo : lo + T // 2])
 
         load_words8(0)
 
@@ -142,6 +145,8 @@ def tile_list_tab48_gelu_kernel(tc, tab, w4_words, w4_scales, tab2, u, b, offs, 
                     )
                     if last:
                         nc.scalar.activation(result[:, lo:hi], acc[g][:], GELU, bias=bias[:])
-                        nc.sync.dma_start(out[:, lo:hi], result[:, lo:hi])
+                        for at, to in STORES:
+                            if lo <= at < hi:
+                                nc.sync.dma_start(out[:, at:to], result[:, at:to])
             if c0 == 0 and a == 0:
                 table4_passes(1)

@@ -78,17 +78,18 @@ def tile_list_tab48_gelu_kernel(tc, tab, w4_words, w4_scales, tab2, u, b, offs, 
             nc.sync.dma_start(rows8[first + ROWS * a : first + ROWS * (a + 1), :], tab_scales[a])
         nc.sync.dma_start(words4[:], tab2[0, 0:WORD_BYTES].rearrange("(p w) -> p w", p=P).bitcast(I32))
         nc.sync.dma_start(u_raw[:], u.rearrange("(a p i) n -> p a i n", p=P, i=PACK))
+
+        def load_words8(a, half):
+            words = tab[a, 0:WORD_BYTES].rearrange("(p w) -> p w", p=P).bitcast(I32)
+            cols = slice(half * T // 2, (half + 1) * T // 2)
+            nc.sync.dma_start(words8[a][:, cols], words[:, cols])
+
+        load_words8(0, 0)
         nc.sync.dma_start(w_words[:], w4_words.rearrange("a p n -> p a n").bitcast(I32))
         for r in range(LIVE):
             nc.sync.dma_start(w_scales[r:P:QUAD, :, :], w4_scale_rows[r:ROWS:LIVE])
         nc.sync.dma_start(bias[:], b.rearrange("(p o) -> p o", o=1))
-
-        def load_words8(a):
-            words = tab[a, 0:WORD_BYTES].rearrange("(p w) -> p w", p=P).bitcast(I32)
-            for lo in range(0, T, T // 2):
-                nc.sync.dma_start(words8[a][:, lo : lo + T // 2], words[:, lo : lo + T // 2])
-
-        load_words8(0)
+        load_words8(0, 1)
 
         nc.vector.memset(rows4[0:first, :], 0)
         nc.vector.memset(rows8[0:first, :], 0)
@@ -105,7 +106,8 @@ def tile_list_tab48_gelu_kernel(tc, tab, w4_words, w4_scales, tab2, u, b, offs, 
                 )
 
         move_rows(0)
-        load_words8(1)
+        load_words8(1, 0)
+        load_words8(1, 1)
         move_rows(1)
 
         nc.scalar.copy(u_bf[:], u_raw[:].rearrange("p a i n -> p a n i"))

@@ -28,7 +28,10 @@ TAB2, TAB = 0, 1
 
 GROUPS = [(0, 256), (256, 512), (512, 768), (768, 896), (896, 1024)]
 STORES = [(lo, lo + 128) for lo in range(0, 512, 128)] + GROUPS[2:]
-GATHERS8 = [(0, 0, 512), (0, 512, 1024)] + [(1, lo, hi) for lo, hi in GROUPS]
+LATE = GROUPS[3][0]
+GATHERS8 = (
+    [(0, 0, LATE)] + [(1, lo, hi) for lo, hi in GROUPS[:3]] + [(0, LATE, S)] + [(1, lo, hi) for lo, hi in GROUPS[3:]]
+)
 
 
 def tile_list_tab48_gelu_kernel(tc, tab, w4_words, w4_scales, tab2, u, b, offs, offs2, out):
@@ -60,10 +63,15 @@ def tile_list_tab48_gelu_kernel(tc, tab, w4_words, w4_scales, tab2, u, b, offs, 
             reused.tile([P, T], I32, name="words8_1", align_bytes=64, offset=16 * S),
         ]
         u_bf = reused.tile([P, PASSES, M, PACK], BF16, name="u_bf", align_bytes=64, offset=8 * S)
-        got8 = [
-            reused.tile([P, S], U32, name="got8_0", align_bytes=64, offset=8 * S),
-            keep.tile([P, S], U32, name="got8_1", align_bytes=64),
-        ]
+        got8_early = reused.tile([P, LATE], U32, name="got8_early", align_bytes=64, offset=8 * S)
+        got8_late = reused.tile([P, PASSES, S - LATE], U32, name="got8_late", align_bytes=64, offset=0)
+        got8_second = keep.tile([P, LATE], U32, name="got8_second", align_bytes=64)
+
+        def got8(a, lo, hi):
+            if lo >= LATE:
+                return got8_late[:, a, lo - LATE : hi - LATE]
+            return got8_second[:, lo:hi] if a == 1 else got8_early[:, lo:hi]
+
         acc = [psum.tile([P, hi - lo], F32, name=f"acc{g}") for g, (lo, hi) in enumerate(GROUPS)]
 
         first = P - PASSES * ROWS
@@ -130,9 +138,10 @@ def tile_list_tab48_gelu_kernel(tc, tab, w4_words, w4_scales, tab2, u, b, offs, 
                 )
 
         table4_passes(0)
+        table4_passes(1)
 
         for a, c0, c1 in GATHERS8:
-            nc.vector.tensor_copy(got8[a][:, c0:c1], words8[a][:].bitcast(U32).indirect(list8[:, c0 // STRIPE : c1 // STRIPE]))
+            nc.vector.tensor_copy(got8(a, c0, c1), words8[a][:].bitcast(U32).indirect(list8[:, c0 // STRIPE : c1 // STRIPE]))
             for g, (lo, hi) in enumerate(GROUPS):
                 if c0 <= lo < c1:
                     last = a == PASSES - 1
@@ -140,7 +149,7 @@ def tile_list_tab48_gelu_kernel(tc, tab, w4_words, w4_scales, tab2, u, b, offs, 
                         out=acc[g][:],
                         lhsT=w_words[:, a, :].bitcast(FP4X4),
                         lhsT_scale=w_scales[:, a, :].bitcast(U8),
-                        rhs=got8[a][:, lo:hi].bitcast(FP8X4),
+                        rhs=got8(a, lo, hi).bitcast(FP8X4),
                         rhs_scale=planes[a][:, TAB, :].bitcast(U8)[:, lo:hi],
                         start=False,
                         stop=last,
@@ -150,5 +159,3 @@ def tile_list_tab48_gelu_kernel(tc, tab, w4_words, w4_scales, tab2, u, b, offs, 
                         for at, to in STORES:
                             if lo <= at < hi:
                                 nc.sync.dma_start(out[:, at:to], result[:, at:to])
-            if c0 == 0 and a == 0:
-                table4_passes(1)

@@ -28,10 +28,6 @@ TAB2, TAB = 0, 1
 
 GROUPS = [(0, 256), (256, 512), (512, 768), (768, 896), (896, 1024)]
 STORES = [(lo, lo + 128) for lo in range(0, 512, 128)] + GROUPS[2:]
-LATE = GROUPS[3][0]
-GATHERS8 = (
-    [(0, 0, LATE)] + [(1, lo, hi) for lo, hi in GROUPS[:3]] + [(0, LATE, S)] + [(1, lo, hi) for lo, hi in GROUPS[3:]]
-)
 
 
 def tile_list_tab48_gelu_kernel(tc, tab, w4_words, w4_scales, tab2, u, b, offs, offs2, out):
@@ -63,14 +59,16 @@ def tile_list_tab48_gelu_kernel(tc, tab, w4_words, w4_scales, tab2, u, b, offs, 
             reused.tile([P, T], I32, name="words8_1", align_bytes=64, offset=16 * S),
         ]
         u_bf = reused.tile([P, PASSES, M, PACK], BF16, name="u_bf", align_bytes=64, offset=8 * S)
-        got8_early = reused.tile([P, LATE], U32, name="got8_early", align_bytes=64, offset=8 * S)
-        got8_late = reused.tile([P, PASSES, S - LATE], U32, name="got8_late", align_bytes=64, offset=0)
-        got8_second = keep.tile([P, LATE], U32, name="got8_second", align_bytes=64)
+        late = GROUPS[-1][0]
+        got8_first = reused.tile([P, late], U32, name="got8_first", align_bytes=64, offset=8 * S)
+        got8_second = reused.tile([P, S], U32, name="got8_second", align_bytes=64, offset=25 * S)
+        got8_head = reused.tile([P, GROUPS[0][1]], U32, name="got8_head", align_bytes=64, offset=24 * S)
+        got8_late = reused.tile([P, S - late], U32, name="got8_late", align_bytes=64, offset=24 * S)
 
         def got8(a, lo, hi):
-            if lo >= LATE:
-                return got8_late[:, a, lo - LATE : hi - LATE]
-            return got8_second[:, lo:hi] if a == 1 else got8_early[:, lo:hi]
+            if a == 0:
+                return got8_first[:, lo:hi] if lo < late else got8_late[:]
+            return got8_second[:, lo:hi] if lo > 0 else got8_head[:]
 
         acc = [psum.tile([P, hi - lo], F32, name=f"acc{g}") for g, (lo, hi) in enumerate(GROUPS)]
 
@@ -125,37 +123,58 @@ def tile_list_tab48_gelu_kernel(tc, tab, w4_words, w4_scales, tab2, u, b, offs, 
         )
         nc.vector.tensor_copy(parted4[:], got4[:].bitcast(U16).rearrange("p (j h) -> p h j", h=PASSES))
 
-        def table4_passes(h):
-            for g, (lo, hi) in enumerate(GROUPS):
-                nc.tensor.matmul_mx(
-                    out=acc[g][:],
-                    lhsT=u_codes[:, h * M : (h + 1) * M].bitcast(FP8X4),
-                    lhsT_scale=u_scales[:, h * M : (h + 1) * M],
-                    rhs=parted4[:, h, lo:hi].bitcast(FP4X4),
-                    rhs_scale=planes[h][:, TAB2, :].bitcast(U8)[:, lo:hi],
-                    start=(h == 0),
-                    stop=False,
-                )
+        def table4_pass(h, g):
+            lo, hi = GROUPS[g]
+            nc.tensor.matmul_mx(
+                out=acc[g][:],
+                lhsT=u_codes[:, h * M : (h + 1) * M].bitcast(FP8X4),
+                lhsT_scale=u_scales[:, h * M : (h + 1) * M],
+                rhs=parted4[:, h, lo:hi].bitcast(FP4X4),
+                rhs_scale=planes[h][:, TAB2, :].bitcast(U8)[:, lo:hi],
+                start=(h == 0),
+                stop=False,
+            )
 
-        table4_passes(0)
-        table4_passes(1)
+        def gather8(a, lo, hi):
+            nc.vector.tensor_copy(got8(a, lo, hi), words8[a][:].bitcast(U32).indirect(list8[:, lo // STRIPE : hi // STRIPE]))
 
-        for a, c0, c1 in GATHERS8:
-            nc.vector.tensor_copy(got8(a, c0, c1), words8[a][:].bitcast(U32).indirect(list8[:, c0 // STRIPE : c1 // STRIPE]))
-            for g, (lo, hi) in enumerate(GROUPS):
-                if c0 <= lo < c1:
-                    last = a == PASSES - 1
-                    nc.tensor.matmul_mx(
-                        out=acc[g][:],
-                        lhsT=w_words[:, a, :].bitcast(FP4X4),
-                        lhsT_scale=w_scales[:, a, :].bitcast(U8),
-                        rhs=got8(a, lo, hi).bitcast(FP8X4),
-                        rhs_scale=planes[a][:, TAB, :].bitcast(U8)[:, lo:hi],
-                        start=False,
-                        stop=last,
-                    )
-                    if last:
-                        nc.scalar.activation(result[:, lo:hi], acc[g][:], GELU, bias=bias[:])
-                        for at, to in STORES:
-                            if lo <= at < hi:
-                                nc.sync.dma_start(out[:, at:to], result[:, at:to])
+        def table8_pass(a, g, closes):
+            lo, hi = GROUPS[g]
+            nc.tensor.matmul_mx(
+                out=acc[g][:],
+                lhsT=w_words[:, a, :].bitcast(FP4X4),
+                lhsT_scale=w_scales[:, a, :].bitcast(U8),
+                rhs=got8(a, lo, hi).bitcast(FP8X4),
+                rhs_scale=planes[a][:, TAB, :].bitcast(U8)[:, lo:hi],
+                start=False,
+                stop=closes,
+            )
+            if closes:
+                nc.scalar.activation(result[:, lo:hi], acc[g][:], GELU, bias=bias[:])
+                for at, to in STORES:
+                    if lo <= at < hi:
+                        nc.sync.dma_start(out[:, at:to], result[:, at:to])
+
+        for g in range(len(GROUPS)):
+            table4_pass(0, g)
+        gather8(0, 0, 512)
+        table8_pass(0, 0, False)
+        table8_pass(0, 1, False)
+        gather8(0, 512, late)
+        for g in range(3):
+            table4_pass(1, g)
+        gather8(1, *GROUPS[0])
+        table8_pass(1, 0, True)
+        table8_pass(0, 2, False)
+        gather8(1, *GROUPS[1])
+        table8_pass(1, 1, True)
+        table4_pass(1, 3)
+        table4_pass(1, 4)
+        table8_pass(0, 3, False)
+        gather8(1, *GROUPS[2])
+        table8_pass(1, 2, True)
+        gather8(1, GROUPS[3][0], S)
+        table8_pass(1, 3, True)
+        table8_pass(1, 4, False)
+        gather8(0, late, S)
+        table8_pass(0, 4, True)

@@ -43,7 +43,7 @@ def tile_list_tab48_gelu_kernel(tc, tab, w4_words, w4_scales, tab2, u, b, offs, 
         words4 = keep.tile([P, T], I32, name="words4", align_bytes=64)
         w_words = keep.tile([P, PASSES, 2 * M // 4], I32, name="w_words", align_bytes=64)
         w_scales = keep.tile([P, PASSES, M // 4], I32, name="w_scales", align_bytes=64)
-        bias = keep.tile([P, 1], F32, name="bias", align_bytes=64)
+        bias = reused.tile([P, 1], F32, name="bias", align_bytes=64, offset=15 * S)
         got_rows = keep.tile([P, 2, S], U8, name="got_rows", align_bytes=64)
         u_codes = keep.tile([P, PASSES * M], U32, name="u_codes", align_bytes=64)
         u_scales = keep.tile([P, PASSES * M], U8, name="u_scales", align_bytes=64)
@@ -53,7 +53,7 @@ def tile_list_tab48_gelu_kernel(tc, tab, w4_words, w4_scales, tab2, u, b, offs, 
 
         u_raw = reused.tile([P, PASSES, PACK, M], F32, name="u_raw", align_bytes=64, offset=0)
         parted4 = reused.tile([P, PASSES, S], U16, name="parted4", align_bytes=64, offset=0)
-        rows8 = reused.tile([P, T // 4], I32, name="rows8", align_bytes=64, offset=16 * S)
+        rows8 = reused.tile([P, T // 4], I32, name="rows8", align_bytes=64, offset=15 * S)
         words8 = [
             keep.tile([P, T], I32, name="words8_0", align_bytes=64),
             reused.tile([P, T], I32, name="words8_1", align_bytes=64, offset=16 * S),
@@ -73,16 +73,18 @@ def tile_list_tab48_gelu_kernel(tc, tab, w4_words, w4_scales, tab2, u, b, offs, 
         acc = [psum.tile([P, hi - lo], F32, name=f"acc{g}") for g, (lo, hi) in enumerate(GROUPS)]
 
         first = P - PASSES * ROWS
-        tab_scales = tab[:, WORD_BYTES:].rearrange("a (q t) -> a q t", t=T).bitcast(I32)
-        tab2_scales = tab2[0, WORD_BYTES:].rearrange("(q t) -> q t", t=T).bitcast(I32)
+        tab_scales = tab[:, WORD_BYTES:].rearrange("a (q t) -> q a t", t=T).bitcast(I32)
+        tab2_scales = tab2[0, WORD_BYTES:].rearrange("(a q t) -> q a t", a=PASSES, t=T).bitcast(I32)
         w4_scale_rows = w4_scales.rearrange("a q n -> q a n").bitcast(I32)
 
         nc.sync.dma_start(rows4[first:P, :], tab2_scales)
         nc.sync.dma_start(list4[:], offs2)
         nc.sync.dma_start(list8[:], offs)
-        for a in range(PASSES):
-            nc.sync.dma_start(rows8[first + ROWS * a : first + ROWS * (a + 1), :], tab_scales[a])
-        nc.sync.dma_start(words4[:], tab2[0, 0:WORD_BYTES].rearrange("(p w) -> p w", p=P).bitcast(I32))
+        nc.sync.dma_start(rows8[first:P, :], tab_scales)
+        tab2_words = tab2[0, 0:WORD_BYTES].rearrange("(p w) -> p w", p=P).bitcast(I32)
+        for half in range(2):
+            cols = slice(half * T // 2, (half + 1) * T // 2)
+            nc.sync.dma_start(words4[:, cols], tab2_words[:, cols])
         nc.sync.dma_start(u_raw[:], u.rearrange("(a p i) n -> p a i n", p=P, i=PACK))
 
         def load_words8(a, half):
@@ -94,7 +96,6 @@ def tile_list_tab48_gelu_kernel(tc, tab, w4_words, w4_scales, tab2, u, b, offs, 
         nc.sync.dma_start(w_words[:], w4_words.rearrange("a p n -> p a n").bitcast(I32))
         for r in range(LIVE):
             nc.sync.dma_start(w_scales[r:P:QUAD, :, :], w4_scale_rows[r:ROWS:LIVE])
-        nc.sync.dma_start(bias[:], b.rearrange("(p o) -> p o", o=1))
         load_words8(0, 1)
 
         nc.vector.memset(rows4[0:first, :], 0)
@@ -105,23 +106,25 @@ def tile_list_tab48_gelu_kernel(tc, tab, w4_words, w4_scales, tab2, u, b, offs, 
         got_rows_words = got_rows[:].rearrange("p t s -> p (t s)").bitcast(I32)
 
         def move_rows(h):
-            row = first + ROWS * h
             for r in range(LIVE):
                 nc.sync.dma_start(
-                    planes[h][r:P:QUAD].rearrange("p t s -> p (t s)"), got_rows_words[row + r : row + ROWS : LIVE, :]
+                    planes[h][r:P:QUAD].rearrange("p t s -> p (t s)"),
+                    got_rows_words[first + PASSES * r + h : P : PASSES * LIVE, :],
                 )
 
         move_rows(0)
         load_words8(1, 0)
-        load_words8(1, 1)
         move_rows(1)
+        load_words8(1, 1)
+        nc.sync.dma_start(bias[:], b.rearrange("(p o) -> p o", o=1))
 
         nc.scalar.copy(u_bf[:], u_raw[:].rearrange("p a i n -> p a n i"))
         nc.vector.tensor_copy(got4[:], words4[:].bitcast(U32).indirect(list4[:]))
         nc.vector.quantize_mx(
             out=u_codes[:].bitcast(FP8X4), scales=u_scales[:], in_=u_bf[:].rearrange("p a n i -> p (a n i)")
         )
-        nc.vector.tensor_copy(parted4[:], got4[:].bitcast(U16).rearrange("p (j h) -> p h j", h=PASSES))
+        for h in range(PASSES):
+            nc.vector.tensor_copy(parted4[:, h, :], got4[:].bitcast(U16).rearrange("p (j h) -> p h j", h=PASSES)[:, h, :])
 
         def table4_pass(h, g):
             lo, hi = GROUPS[g]
@@ -155,26 +158,18 @@ def tile_list_tab48_gelu_kernel(tc, tab, w4_words, w4_scales, tab2, u, b, offs, 
                     if lo <= at < hi:
                         nc.sync.dma_start(out[:, at:to], result[:, at:to])
 
-        for g in range(len(GROUPS)):
-            table4_pass(0, g)
-        gather8(0, 0, 512)
-        table8_pass(0, 0, False)
-        table8_pass(0, 1, False)
-        gather8(0, 512, late)
-        for g in range(3):
-            table4_pass(1, g)
-        gather8(1, *GROUPS[0])
-        table8_pass(1, 0, True)
-        table8_pass(0, 2, False)
-        gather8(1, *GROUPS[1])
-        table8_pass(1, 1, True)
-        table4_pass(1, 3)
-        table4_pass(1, 4)
-        table8_pass(0, 3, False)
-        gather8(1, *GROUPS[2])
-        table8_pass(1, 2, True)
-        gather8(1, GROUPS[3][0], S)
-        table8_pass(1, 3, True)
-        table8_pass(1, 4, False)
+        last = len(GROUPS) - 1
+        for h in range(PASSES):
+            for g in range(len(GROUPS)):
+                table4_pass(h, g)
+        gather8(0, 0, late)
+        for g in range(last):
+            table8_pass(0, g, False)
+        for g in range(last - 1):
+            gather8(1, *GROUPS[g])
+            table8_pass(1, g, True)
+        gather8(1, GROUPS[last - 1][0], S)
+        table8_pass(1, last - 1, True)
+        table8_pass(1, last, False)
         gather8(0, late, S)
-        table8_pass(0, 4, True)
+        table8_pass(0, last, True)

from contextlib import ExitStack

import concourse.mybir as mybir

K, L, M, T, S = 1024, 1024, 128, 2048, 1024
FLOPS = 2 * (K + L) * M * S

F32 = mybir.dt.float32
BF16 = mybir.dt.bfloat16
I32 = mybir.dt.int32
U32 = mybir.dt.uint32
U16 = mybir.dt.uint16
U8 = mybir.dt.uint8
FP8X4 = mybir.dt.float8_e4m3fn_x4
FP4X4 = mybir.dt.float4_e2m1fn_x4
GELU = mybir.ActivationFunctionType.Gelu_apprx_tanh

P = 128
PACK = 4
PASSES = 2
QUADS = 4
QUAD = 32
LIVE = 4
ROWS = QUADS * LIVE
STRIPE = 16
WORD_BYTES = P * PACK * T
TAB2, TAB = 0, 1

GROUPS = [(0, 256), (256, 512), (512, 768), (768, 896), (896, 1024)]
STORES = [(lo, lo + 128) for lo in range(0, 512, 128)] + GROUPS[2:]


def tile_list_tab48_gelu_kernel(tc, tab, w4_words, w4_scales, tab2, u, b, offs, offs2, out):
    nc = tc.nc
    with ExitStack() as ctx:
        keep = ctx.enter_context(tc.tile_pool(name="keep", bufs=1))
        reused = ctx.enter_context(tc.tile_pool(name="reused", bufs=1))
        psum = ctx.enter_context(tc.psum_pool(name="psum", bufs=1))

        list8 = keep.tile([P, S // STRIPE], U16, name="list8")
        list4 = keep.tile([P, S // STRIPE], U16, name="list4")
        rows4 = keep.tile([P, T // 4], I32, name="rows4", align_bytes=64)
        words4 = keep.tile([P, T], I32, name="words4", align_bytes=64)
        w_words = keep.tile([P, PASSES, 2 * M // 4], I32, name="w_words", align_bytes=64)
        w_scales = keep.tile([P, PASSES, M // 4], I32, name="w_scales", align_bytes=64)
        bias = reused.tile([P, 1], F32, name="bias", align_bytes=64, offset=15 * S)
        got_rows = keep.tile([P, 2, S], U8, name="got_rows", align_bytes=64)
        u_codes = keep.tile([P, PASSES * M], U32, name="u_codes", align_bytes=64)
        u_scales = keep.tile([P, PASSES * M], U8, name="u_scales", align_bytes=64)
        planes = [keep.tile([P, 2, S // 4], I32, name=f"planes{h}", align_bytes=64) for h in range(PASSES)]
        got4 = keep.tile([P, S], U32, name="got4", align_bytes=64)
        result = keep.tile([P, S], F32, name="result", align_bytes=64)

        u_raw = reused.tile([P, PASSES, PACK, M], F32, name="u_raw", align_bytes=64, offset=0)
        parted4 = reused.tile([P, PASSES, S], U16, name="parted4", align_bytes=64, offset=0)
        rows8 = reused.tile([P, T // 4], I32, name="rows8", align_bytes=64, offset=15 * S)
        words8 = [
            keep.tile([P, T], I32, name="words8_0", align_bytes=64),
            reused.tile([P, T], I32, name="words8_1", align_bytes=64, offset=16 * S),
        ]
        u_bf = reused.tile([P, PASSES, M, PACK], BF16, name="u_bf", align_bytes=64, offset=8 * S)
        late = GROUPS[-1][0]
        got8_first = reused.tile([P, late], U32, name="got8_first", align_bytes=64, offset=8 * S)
        got8_second = reused.tile([P, S], U32, name="got8_second", align_bytes=64, offset=25 * S)
        got8_head = reused.tile([P, GROUPS[0][1]], U32, name="got8_head", align_bytes=64, offset=24 * S)
        got8_late = reused.tile([P, S - late], U32, name="got8_late", align_bytes=64, offset=24 * S)

        def got8(a, lo, hi):
            if a == 0:
                return got8_first[:, lo:hi] if lo < late else got8_late[:]
            return got8_second[:, lo:hi] if lo > 0 else got8_head[:]

        acc = [psum.tile([P, hi - lo], F32, name=f"acc{g}") for g, (lo, hi) in enumerate(GROUPS)]

        first = P - PASSES * ROWS
        tab_scales = tab[:, WORD_BYTES:].rearrange("a (q t) -> q a t", t=T).bitcast(I32)
        tab2_scales = tab2[0, WORD_BYTES:].rearrange("(a q t) -> q a t", a=PASSES, t=T).bitcast(I32)
        w4_scale_rows = w4_scales.rearrange("a q n -> q a n").bitcast(I32)

        nc.sync.dma_start(rows4[first:P, :], tab2_scales)
        nc.sync.dma_start(list4[:], offs2)
        nc.sync.dma_start(list8[:], offs)
        nc.sync.dma_start(rows8[first:P, :], tab_scales)
        tab2_words = tab2[0, 0:WORD_BYTES].rearrange("(p w) -> p w", p=P).bitcast(I32)
        for half in range(2):
            cols = slice(half * T // 2, (half + 1) * T // 2)
            nc.sync.dma_start(words4[:, cols], tab2_words[:, cols])
        nc.sync.dma_start(u_raw[:], u.rearrange("(a p i) n -> p a i n", p=P, i=PACK))

        def load_words8(a, half):
            words = tab[a, 0:WORD_BYTES].rearrange("(p w) -> p w", p=P).bitcast(I32)
            cols = slice(half * T // 2, (half + 1) * T // 2)
            nc.sync.dma_start(words8[a][:, cols], words[:, cols])

        load_words8(0, 0)
        nc.sync.dma_start(w_words[:], w4_words.rearrange("a p n -> p a n").bitcast(I32))
        for r in range(LIVE):
            nc.sync.dma_start(w_scales[r:P:QUAD, :, :], w4_scale_rows[r:ROWS:LIVE])
        load_words8(0, 1)

        nc.vector.memset(rows4[0:first, :], 0)
        nc.vector.memset(rows8[0:first, :], 0)

        nc.vector.tensor_copy(got_rows[:, TAB2, :], rows4[:].bitcast(U8).indirect(list4[:]))
        nc.vector.tensor_copy(got_rows[:, TAB, :], rows8[:].bitcast(U8).indirect(list8[:]))
        got_rows_words = got_rows[:].rearrange("p t s -> p (t s)").bitcast(I32)

        def move_rows(h):
            for r in range(LIVE):
                nc.sync.dma_start(
                    planes[h][r:P:QUAD].rearrange("p t s -> p (t s)"),
                    got_rows_words[first + PASSES * r + h : P : PASSES * LIVE, :],
                )

        move_rows(0)
        load_words8(1, 0)
        move_rows(1)
        load_words8(1, 1)
        nc.sync.dma_start(bias[:], b.rearrange("(p o) -> p o", o=1))

        nc.scalar.copy(u_bf[:], u_raw[:].rearrange("p a i n -> p a n i"))
        nc.vector.tensor_copy(got4[:], words4[:].bitcast(U32).indirect(list4[:]))
        nc.vector.quantize_mx(
            out=u_codes[:].bitcast(FP8X4), scales=u_scales[:], in_=u_bf[:].rearrange("p a n i -> p (a n i)")
        )
        for h in range(PASSES):
            nc.vector.tensor_copy(parted4[:, h, :], got4[:].bitcast(U16).rearrange("p (j h) -> p h j", h=PASSES)[:, h, :])

        def table4_pass(h, g):
            lo, hi = GROUPS[g]
            nc.tensor.matmul_mx(
                out=acc[g][:],
                lhsT=u_codes[:, h * M : (h + 1) * M].bitcast(FP8X4),
                lhsT_scale=u_scales[:, h * M : (h + 1) * M],
                rhs=parted4[:, h, lo:hi].bitcast(FP4X4),
                rhs_scale=planes[h][:, TAB2, :].bitcast(U8)[:, lo:hi],
                start=(h == 0),
                stop=False,
            )

        def gather8(a, lo, hi):
            nc.vector.tensor_copy(got8(a, lo, hi), words8[a][:].bitcast(U32).indirect(list8[:, lo // STRIPE : hi // STRIPE]))

        def table8_pass(a, g, closes):
            lo, hi = GROUPS[g]
            nc.tensor.matmul_mx(
                out=acc[g][:],
                lhsT=w_words[:, a, :].bitcast(FP4X4),
                lhsT_scale=w_scales[:, a, :].bitcast(U8),
                rhs=got8(a, lo, hi).bitcast(FP8X4),
                rhs_scale=planes[a][:, TAB, :].bitcast(U8)[:, lo:hi],
                start=False,
                stop=closes,
            )
            if closes:
                nc.scalar.activation(result[:, lo:hi], acc[g][:], GELU, bias=bias[:])
                for at, to in STORES:
                    if lo <= at < hi:
                        nc.sync.dma_start(out[:, at:to], result[:, at:to])

        last = len(GROUPS) - 1
        for h in range(PASSES):
            for g in range(len(GROUPS)):
                table4_pass(h, g)
        gather8(0, 0, late)
        for g in range(last):
            table8_pass(0, g, False)
        for g in range(last - 1):
            gather8(1, *GROUPS[g])
            table8_pass(1, g, True)
        gather8(1, GROUPS[last - 1][0], S)
        table8_pass(1, last - 1, True)
        table8_pass(1, last, False)
        gather8(0, late, S)
        table8_pass(0, last, True)
